import numpy as np, ml_dtypes
CORES = [35,38,43,46]
N = 4
BF = ml_dtypes.bfloat16
def f(rng, *shape):
    return (rng.standard_normal(shape, dtype=np.float32) * np.exp2(rng.integers(-2, 3, shape[:-1] + (1,)))).astype(BF)
def wide(rng, *shape):
    v = f(rng, *shape).astype(np.float32); k = shape[:-2] + (1, shape[-1])
    return (v * np.exp2(rng.integers(-6, 7, k)) * (rng.random(k) > 0.0625)).astype(BF)
def gentries(a):
    return np.ascontiguousarray(a.reshape(8, 16, -1).transpose(0, 2, 1)).reshape(8, -1)
def gtable(e):
    e = np.asarray(e); return np.ascontiguousarray(e.reshape(8, -1, 16).transpose(0, 2, 1)).reshape(128, -1).astype(np.int32)
Q, CAPP, M, E, D = 512, 160, 4096, 8192, 4
LV, L = [1, 15, 210, 1900], 4000
EMPTY = 2 ** 24 - 1
def cut(rng, n, m, cap, s):
    u = rng.random((m, cap - 1)) + s * rng.random((m, 1))
    return 1 + np.bincount(np.argsort(u.reshape(-1))[:n - m] // (cap - 1), minlength=m)
def tree(rng, lv, n, keys, repeat=False):
    nk = np.sort(rng.integers(0, EMPTY - 16, (16, M)), axis=0) + np.arange(16)[:, None]
    nk[np.arange(16)[:, None] >= rng.integers(1, 17, (1, M))] = EMPTY
    beg = rng.integers(0, E - 15, M); kid = rng.integers(0, M, E)
    ids = np.concatenate([[0], 1 + rng.permutation(M - 1)]); a = np.cumsum([0] + list(lv))
    lev = [ids[a[l]:a[l + 1]] for l in range(D)]; nxt = lev[1:] + [rng.integers(0, M, n) if repeat else rng.permutation(M)[:n]]
    ek = np.asarray(keys); sizes = []
    for l in range(D - 1, -1, -1):
        sz = cut(rng, len(ek), lv[l], 16, 2.0); st = np.cumsum(sz) - sz
        nk[:, lev[l]] = EMPTY; nk[np.arange(len(ek)) - np.repeat(st, sz), np.repeat(lev[l], sz)] = ek
        ek = ek[st]; sizes.insert(0, sz)
    S = np.concatenate(sizes); C = np.concatenate(nxt); t = len(C); m = len(S)
    o = rng.permutation(m); so = S[o]; st = np.zeros(m, np.int64)
    st[o] = np.cumsum(so) - so + np.sort(rng.integers(0, E - 16 - t + 1, m))
    beg[ids[:m]] = st; kid[np.repeat(st - (np.cumsum(S) - S), S) + np.arange(t)] = C
    return nk, beg, kid
def make(rng, shapes=None, ends=False, full=False, alike=False, repeat=False):
    shapes = shapes or [(LV, L)] * N; I = np.int32
    spl = np.sort(rng.integers(0, EMPTY - 16384 * N + 1, (8, N - 1)), axis=1) + 16384 * np.arange(1, N)
    spl = np.concatenate([np.zeros((8, 1), np.int64), spl], axis=1); hi = np.concatenate([spl[:, 1:], np.full((8, 1), EMPTY)], axis=1)
    nk = np.zeros((N, 128, M), I); beg = np.zeros((N, 8, M), I); kid = np.zeros((N, 8, E), I); sk = np.zeros((N, 8, M), np.int64); ln = np.array([n for _, n in shapes])
    for r in range(N):
        lv, n = shapes[r]
        for g in range(8):
            w = int(hi[g, r] - spl[g, r])
            if ends: k = np.arange(n) + (w - n) * (r % 2)
            else: k = np.sort(rng.integers(0, w - n + 1, n)) + np.arange(n)
            k[0] = 0; k = k + spl[g, r]; sk[r, g, :n] = k
            nk[r, 16 * g:16 * g + 16], beg[r, g], kid[r, g] = tree(rng, lv, n, k, repeat)
    q = np.zeros((N, 8, Q), np.int64)
    for r in range(N):
        for g in range(8):
            if full: cn = np.zeros(N, np.int64); cn[rng.permutation(N)] = np.clip(Q - CAPP * np.arange(N), 0, CAPP)
            else: cn = 3 + cut(rng, Q - 3 * N, N, CAPP - 3, 0.5)
            own = np.repeat(np.arange(N), cn); st = np.cumsum(cn) - cn; occ = np.arange(Q) - st[own]
            a = spl[g, own]; b = hi[g, own]; k = sk[own, g, np.floor(rng.random(Q) * ln[own]).astype(np.int64)]
            inside = a + np.floor(rng.random(Q) * (b - a)).astype(np.int64)
            kd = 1 + occ % 4 if ends else np.array([0, 0, 0, 0, 0, 1, 1, 1, 2, 2, 2, 3, 4])[rng.integers(0, 13, Q)]
            v = np.choose(kd, [inside, k, np.maximum(k - 1, a), a, b - 1])
            if alike: v = v[st[own]]
            q[r, g] = v[rng.permutation(Q)]
    return {"nk": nk, "beg": beg, "kid": kid, "vec": f(rng, N, 128, M), "spl": np.stack([spl.astype(I)] * N), "q": np.stack([gtable(x) for x in q])}
def setup_inputs(rng):
    return make(rng)
def setup_inputs_caps(rng):
    return make(rng, full=True)
def setup_inputs_ends(rng):
    return make(rng, ends=True)
def setup_inputs_shapes(rng):
    a = []; n = M
    for l in range(D): n = -(-n // 16); a.insert(0, n)
    k = M * 3 // 8; b = [min(16 ** l, k) for l in range(D)]; s = int(rng.integers(0, 2))
    return make(rng, shapes=[(a, M) if (r + s) % 2 else (b, k) for r in range(N)], repeat=True)
def setup_inputs_alike(rng):
    return make(rng, alike=True)
def setup_inputs_spread(rng):
    d = make(rng); d["vec"] = wide(rng, N, 128, M); return d
def check_inputs(d):
    bad = []; nk, beg, kid, spl, q = [np.asarray(d[x]).astype(np.int64) for x in ("nk", "beg", "kid", "spl", "q")]
    if not np.isfinite(np.asarray(d["vec"]).astype(np.float32)).all(): bad.append("finite")
    if any(bool((a < 0).any() or (a > b).any()) for a, b in ((nk, EMPTY), (beg, E - 16), (kid, M - 1), (spl, EMPTY - 1), (q, EMPTY - 1))): return bad + ["ranges"]
    if (spl != spl[:1]).any() or (spl[:, :, 0] != 0).any() or (np.diff(spl, axis=2) <= 0).any(): return bad + ["splitters"]
    n4 = nk.reshape(N, 8, 16, M)
    if ((n4[:, :, 1:] <= n4[:, :, :-1]) & (n4[:, :, 1:] < EMPTY)).any(): bad.append("nodes")
    ok = True
    for r in range(N):
        for g in range(8):
            nd = np.zeros(1, np.int64); ek = spl[r, g, r:r + 1]; seen = [nd]
            for l in range(D):
                k = n4[r, g][:, nd].T
                if len(nd) > M or (k[:, 0] != ek).any(): ok = False; break
                use = k < EMPTY; ek = k[use]; nd = kid[r, g][(beg[r, g][nd][:, None] + np.arange(16))[use]]
                if l < D - 1:
                    seen.append(nd)
                    if len(nd) > M: ok = False; break
            if not ok: break
            s = np.concatenate(seen); top = spl[r, g, r + 1] if r + 1 < N else EMPTY
            if len(np.unique(s)) != len(s) or (np.diff(ek) <= 0).any() or ek[-1] >= top: ok = False
        if not ok: break
    if not ok: bad.append("tree")
    for r in range(N):
        x = gentries(q[r]); own = np.sum(x[:, :, None] >= spl[r][:, None, :], axis=2) - 1
        if any(np.bincount(own[g], minlength=N).max() > CAPP for g in range(8)): bad.append("caps"); break
    return bad
def reference(nk, beg, kid, vec, spl, q):
    y = np.zeros((N, 128, Q), vec.dtype); G = np.arange(8)[:, None]
    n4 = nk.reshape(N, 8, 16, M); v4 = vec.reshape(N, 8, 16, M)
    for r in range(N):
        x = gentries(q[r])
        own = np.sum(x[:, :, None] >= spl[r][:, None, :], axis=2) - 1
        at = np.zeros((8, Q), np.int64)
        for l in range(D):
            c = np.sum(n4[own, G, :, at] <= x[:, :, None], axis=2)
            at = kid[own, G, beg[own, G, at] + c - 1]
        y[r] = v4[own, G, :, at].transpose(0, 2, 1).reshape(128, Q)
    return {"y": y}

@@ -1,0 +1,312 @@
+from concourse.bass import DstId, RemoteDMATransfer
+from concourse.mybir import dt, AluOpType, AxisListType, ActivationFunctionType
+
+CAP = 160
+NQ = 640
+NS = 128
+
+SCRATCH = {
+    "spi": ("sbuf", [8, 4], "int32"),
+    "spf": ("sbuf", [8, 4], "float32"),
+    "onef": ("sbuf", [8, 128], "float32"),
+    "R8a": ("sbuf", [8, 128], "float32"),
+    "R8": ("sbuf", [8, 128], "float32"),
+}
+for _dt, _bufs in (
+    ("int32", "ql 32 X0 512 nks 4096 C 768 k1i 2 pid 1 pim 1 SX 640 QX 640 K2 16 K3 256"),
+    ("float32", "k1f 1 ioI 1 INC 128 U 128"),
+    ("bfloat16", "vcs 4096 BK 8192 CH 768 CL 768 ones 160 BDa 128 BD 128 NU 128 RBa 128 RB 128 CB 128 RST 128 DD 160 D0 160 D1 160 "
+                 "wt 48 Wk 144 Wb 144 Wc 144 W16 144 GE 160 MK 128 kg16 16 b2 16 kg256 256 b3w 256 cm1 640 cm2 640 cm3 640 cm4 640 "
+                 "bg3 640 bg4 640 kg3 640 kg4 640 AN 640 RX 640 yb 512"),
+    ("float16", "D0h 160 D1h 160 VAL 128 F1 64 SL 32 TT 32"),
+    ("uint16", "LA 32 LB 32 L16 2 LM2 2 L256 16 LM3 16 l1 40 l2 40 i3 40 m4 40 i4 40 vn 40"),
+):
+    _w = _bufs.split()
+    for _k in range(0, len(_w), 2):
+        SCRATCH[_w[_k]] = ("sbuf", [128, int(_w[_k + 1])], _dt)
+for _k in "pS pT pN pA p1 p2 pC pD".split():
+    SCRATCH[_k] = ("psum", [128, 512], "float32")
+SEMAPHORES = ["s%d" % i for i in range(NS)] + ["rq%d" % i for i in range(4)] + ["ra%d" % i for i in range(4)] + ["lq", "la"]
+
+A = AluOpType
+COPY = ActivationFunctionType.Copy
+
+
+def rank_program(g, core, T, topo):
+    me = T.rank_of(core)
+    if me is None:
+        return
+    v, s, te, sy = g.vector, g.scalar, g.tensor, g.sync
+    queues = {"g": g, "v": v, "s": s, "t": te, "y": sy}
+    used = [0]
+    seen = {}
+    waited = {}
+    every = []
+
+    def incs(*ins, n=1):
+        name = "s%d" % used[0]
+        used[0] += 1
+        for x in ins:
+            x.then_inc(T.sem[name], n)
+        tok = (name, n * len(ins))
+        every.append(tok)
+        return tok
+
+    def dmas(*calls):
+        return incs(*[q.dma_start(out, in_) for q, out, in_ in calls], n=16)
+
+    def W(key, *toks):
+        for tok in toks:
+            if (key, tok) in seen:
+                continue
+            seen[(key, tok)] = True
+            waited[tok] = True
+            queues[key].wait_ge(T.sem[tok[0]], tok[1])
+
+    def conv(out, wt, src, n, start=True, stop=True):
+        ins = None
+        for i in range(16):
+            ins = te.matmul(out, wt[:, 15 - i:143 - i], src[:, i:n:16], start and i == 0, stop and i == 15)
+        return ins
+
+    d_ql = dmas((sy, T.ql[:], T.q[:]))
+    d_sp = dmas((s, T.spi[:], T.spl[:]))
+    d_c = dmas((sy, T.C[:, 0:512], T.kid[:]), (sy, T.C[:, 512:768], T.beg[:]))
+    d_k1 = dmas((s, T.k1i[:], T.nk[:, 0:2]))
+    d_x0 = dmas(*[((sy, s)[o % 2], T.X0[o::16, :], T.q[:]) for o in range(16)])
+    d_na = dmas((sy, T.nks[0:64, :], T.nk[0:64, :]))
+
+    t_onef = incs(v.memset(T.onef[:], 1.0))
+    t_ones = incs(v.memset(T.ones[:], 1.0))
+    t_bk0 = incs(v.memset(T.BK[:, 0:2048], 0.0))
+    t_w0 = incs(*[v.memset(x[:], 0.0) for x in (T.Wk, T.Wb, T.Wc)])
+    t_ge0 = incs(v.memset(T.GE[:, 0:32], 1.0), v.memset(T.GE[:, 128:160], 0.0))
+    t_bk1 = incs(v.memset(T.BK[:, 2048:4096], 0.0))
+    t_sx = incs(v.memset(T.SX[:], 0))
+    W("s", t_bk0)
+    t_bk2 = incs(*[s.activation(T.BK[:, b:b + 2048], T.BK[:, 0:2048], COPY) for b in (4096, 6144)])
+
+    def sel(out, in_, pattern, op, base, cm, *deps):
+        W("g", *deps)
+        return incs(g.affine_select(out, in_, pattern, op, 0.0, base, cm))
+
+    c = sel(T.R8a[:], T.onef[:], [[1, 128]], A.is_ge, 0, -16, t_onef)
+    c_r8 = sel(T.R8[:], T.R8a[:], [[-1, 128]], A.is_ge, 15, 16, c)
+    c_bda = sel(T.BDa[:], T.ones[:, 0:128], [[16, 8], [0, 16]], A.is_ge, 15, -1, t_ones)
+    c_bd = sel(T.BD[:], T.BDa[:], [[-16, 8], [0, 16]], A.is_ge, 0, 1, c_bda)
+    c_rst = sel(T.RST[:], T.ones[:, 0:128], [[0, 4], [1, 32]], A.is_gt, 0, 0, t_ones)
+    c_cb = incs(g.iota(T.CB[:], [[-10, 4], [0, 32]], 0, 0, allow_small_or_imprecise_dtypes=True))
+    c_nu = sel(T.NU[:], T.BDa[:], [[-16, 8], [-1, 16]], A.is_ge, 0, 1, c_bda)
+    c_dd = sel(T.DD[:], T.ones[:], [[-1, 160]], A.is_equal, 16, 1, t_ones)
+    c_d0 = sel(T.D0[:], T.DD[:], [[0, 5], [1, 32]], A.is_ge, -16, 0, c_dd)
+    c_d1 = sel(T.D1[:], T.DD[:], [[0, 5], [-1, 32]], A.is_ge, 15, 0, c_dd)
+    c_pid = incs(g.iota(T.pid[:], [[0, 1]], 0, 1))
+    wts = []
+    for k, (w, lo, hi) in enumerate(((T.Wk, 0, 1), (T.Wb, 2, 3), (T.Wc, 1, 15))):
+        c = sel(T.wt[:, 16 * k:16 * k + 9], T.ones[:, 0:9], [[-16, 9]], A.is_ge, -lo, 1, t_ones)
+        wts.append(sel(w[:, 15:144:16], T.wt[:, 16 * k:16 * k + 9], [[16, 9]], A.is_ge, hi, -1, c, t_w0))
+    c_wk, c_wb, c_wc = wts
+    c = sel(T.RBa[:], T.ones[:, 0:128], [[16, 8], [0, 16]], A.is_ge, 3, -1, t_ones)
+    c_rb = sel(T.RB[:], T.RBa[:], [[-16, 8], [0, 16]], A.is_ge, -2, 1, c)
+
+    W("v", d_sp)
+    t_spf = incs(v.tensor_copy(T.spf[:], T.spi[:]))
+    W("t", t_spf, c_r8)
+    p_sp = incs(te.matmul(T.pS[:, 0:4], T.R8[:], T.spf[:], True, True))
+    W("v", d_ql, p_sp)
+    t_ge = incs(*[v.tensor_scalar(T.GE[:, 32 * r:32 * r + 32], T.ql[:], T.pS[:, r:r + 1], None, A.is_ge) for r in (1, 2, 3)])
+    W("v", t_ge, t_ge0)
+    t_mk = incs(v.tensor_tensor(T.MK[:], T.GE[:, 0:128], T.GE[:, 32:160], A.subtract))
+    W("t", c_bd, c_cb)
+    te.matmul(T.pN[:, 0:128], T.BD[:], T.CB[:], True, False)
+    W("t", t_mk)
+    p_t1 = incs(te.matmul(T.pT[:, 0:128], T.BD[:], T.MK[:], True, True))
+    W("t", c_nu)
+    p_n = incs(te.matmul(T.pN[:, 0:128], T.NU[:], T.MK[:], False, True))
+    W("v", d_c)
+    t_ch = incs(v.tensor_copy(T.CH[:], T.C[:]))
+    W("v", p_t1, c_rst)
+    t_inc = incs(v.tensor_tensor_scan(T.INC[:], T.RST[:], T.pT[:, 0:128], 0.0, A.mult, A.add))
+    W("v", t_inc, p_n)
+    t_u = incs(v.tensor_tensor(T.U[:], T.INC[:], T.pN[:, 0:128], A.subtract))
+    W("v", t_u, t_mk)
+    t_val = incs(v.tensor_tensor(T.VAL[:], T.MK[:], T.U[:], A.mult))
+    W("v", t_val)
+    t_f1 = incs(v.tensor_tensor(T.F1[:], T.VAL[:, 0:64], T.VAL[:, 64:128], A.add))
+    W("v", t_f1)
+    t_sl = incs(v.tensor_tensor(T.SL[:], T.F1[:, 0:32], T.F1[:, 32:64], A.add))
+    W("v", t_sl)
+    t_tt = incs(v.transpose(T.TT[:], T.SL[:]))
+    W("v", c_d0, c_d1)
+    t_dh = incs(v.tensor_copy(T.D0h[:], T.D0[:]), v.tensor_copy(T.D1h[:], T.D1[:]))
+    W("t", t_tt, t_dh)
+    p_a = []
+    for w in range(2):
+        for gg in range(2):
+            sh = 16 + 16 * (w - gg)
+            p_a.append(te.matmul(T.pA[:, w:32:2], (T.D0h, T.D1h)[w][:, sh:sh + 128], T.TT[:, 16 * gg:16 * gg + 16], gg == 0, gg == 1))
+    p_a = incs(*p_a[1::2])
+    W("v", t_ch)
+    t_cl = incs(v.tensor_tensor(T.CL[:], T.C[:], T.CH[:], A.subtract))
+    W("v", p_a)
+    t_la = incs(v.tensor_copy(T.LA[:], T.pA[:, 0:32]))
+    W("v", t_la, d_x0, t_sx)
+    t_sc = incs(v.tensor_copy(T.SX[:, 0:640].indirect(T.LA[:, 0:32]), T.X0[:]))
+
+    W("y", t_ch, t_cl, t_bk0, t_bk1, t_bk2)
+    d_bk = dmas((sy, T.BK[0::16, :], T.CH[:, 0:512]), (sy, T.BK[2::16, 0:4096], T.CH[:, 512:768]),
+                (sy, T.BK[1::16, :], T.CL[:, 0:512]), (sy, T.BK[3::16, 0:4096], T.CL[:, 512:768]))
+    d_nb = dmas((sy, T.nks[64:128, :], T.nk[64:128, :]))
+
+    def engines_of(src, dst):
+        away = [d for d in T.cores if topo.chip(d) != topo.chip(src)]
+        ae = topo.engines(src, away[0])
+        if dst in away:
+            n = len(ae) // len(away)
+            return ae[away.index(dst) * n:away.index(dst) * n + n]
+        return [e for e in topo.engines(src, dst) if e not in ae]
+
+    def count(r):
+        return len(engines_of(T.cores[r], core))
+
+    others = sorted([r for r in range(4) if r != me], key=lambda r: topo.chip(T.cores[r]) != topo.chip(core))
+
+    def exchange(src, dst, sem, lsem):
+        tr = []
+        for r in others:
+            d = T.cores[r]
+            a = topo.addr(d)
+            tr.append(RemoteDMATransfer(dst_ids=[DstId(rid=a[0], pnc=a[1])], dma_engine_mask=sum(1 << e for e in engines_of(core, d)),
+                                        remote_sem=T.sem["%s%d" % (sem, me)], src=src[:, CAP * r:CAP * r + CAP],
+                                        dst=dst[:, CAP * me:CAP * me + CAP]))
+        g.remote_dma_fused(tr, local_sem=T.sem[lsem])
+        return sum(len(engines_of(core, T.cores[r])) for r in others)
+
+    W("g", t_sc)
+    n_lq = exchange(T.SX, T.QX, "rq", "lq")
+
+    W("v", t_sc)
+    own = slice(CAP * me, CAP * me + CAP)
+    t_ox = incs(v.tensor_copy(T.QX[:, own], T.SX[:, own]))
+    W("v", d_k1)
+    t_k1 = incs(v.tensor_copy(T.k1f[:], T.k1i[:, 0:1]))
+    W("v", c_pid)
+    t_pim = incs(v.tensor_scalar(T.pim[:], T.pid[:], 15, None, A.bitwise_and))
+    W("v", t_pim)
+    t_io = incs(v.tensor_copy(T.ioI[:], T.pim[:]))
+    W("v", c_wc)
+    t_w16 = incs(v.tensor_scalar(T.W16[:], T.Wc[:], 16.0, None, A.mult))
+    t_lb = incs(v.tensor_copy(T.LB[:], T.SL[:]))
+    W("v", t_k1, t_ox)
+    t_c1o = incs(v.tensor_scalar(T.cm1[:, own], T.QX[:, own], T.k1f[:, 0:1], None, A.is_ge))
+    W("t", d_bk, c_rb)
+    p_b0 = incs(te.matmul(T.p1[:, 0:1], T.RB[:], T.BK[:, 0:1], True, True))
+    W("v", p_b0, t_io)
+    t_l16 = incs(v.tensor_scalar(T.L16[:, 0:1], T.p1[:, 0:1], T.ioI[:, 0:1], None, A.add))
+    W("s", t_l16, d_bk)
+    s_k16 = incs(s.activation(T.kg16[:], T.BK[:, 0:8192].indirect(T.L16[:, 0:1]), COPY))
+    W("t", s_k16, c_wk)
+    p_m2 = incs(conv(T.p2[:, 0:1], T.Wk, T.kg16, 16))
+    W("v", p_m2)
+    t_m2 = incs(v.tensor_copy(T.LM2[:, 0:1], T.p2[:, 0:1]))
+    W("s", t_m2)
+    s_b2 = incs(s.activation(T.b2[:], T.BK[:, 0:4096].indirect(T.LM2[:, 0:1]), COPY))
+    W("t", s_b2, t_l16)
+    p_b2 = incs(te.matmul(T.p1[:, 0:16], T.RB[:], T.b2[:], True, True))
+    W("v", p_b2)
+    t_l256 = incs(v.tensor_scalar(T.L256[:], T.p1[:, 0:16], T.ioI[:, 0:1], None, A.add))
+    W("s", t_l256)
+    s_k256 = incs(s.activation(T.kg256[:], T.BK[:, 0:8192].indirect(T.L256[:, 0:16]), COPY))
+    W("v", d_na, d_nb, t_m2)
+    t_k2 = incs(v.tensor_copy(T.K2[:], T.nks[:, 0:4096].indirect(T.LM2[:, 0:1])))
+    W("t", s_k256, t_m2)
+    p_m3 = incs(conv(T.p2[:, 0:16], T.Wk, T.kg256, 256))
+    W("v", p_m3)
+    t_m3 = incs(v.tensor_copy(T.LM3[:], T.p2[:, 0:16]))
+    W("s", t_m3)
+    s_b3 = incs(s.activation(T.b3w[:], T.BK[:, 0:4096].indirect(T.LM3[:, 0:16]), COPY))
+    W("v", t_m3)
+    t_k3 = incs(v.tensor_copy(T.K3[:], T.nks[:, 0:4096].indirect(T.LM3[:, 0:16])))
+
+    t_c1 = []
+    for r in others:
+        v.wait_ge(T.sem["rq%d" % r], count(r))
+        b = slice(CAP * r, CAP * r + CAP)
+        t_c1.append(v.tensor_scalar(T.cm1[:, b], T.QX[:, b], T.k1f[:, 0:1], None, A.is_ge))
+    t_c1 = incs(*t_c1)
+    W("y", t_c1)
+    d_vec = dmas((sy, T.vcs[:], T.vec[:]))
+    W("t", c_wc, t_c1, t_c1o)
+    p_1 = incs(conv(T.pC[:, 0:40], T.Wc, T.cm1, NQ))
+    W("t", t_w16)
+    conv(T.pD[:, 0:40], T.W16, T.cm1, NQ, True, False)
+    W("v", p_1)
+    t_l1 = incs(v.tensor_copy(T.l1[:], T.pC[:, 0:40]))
+    W("v", t_l1, t_k2)
+    t_c2 = incs(v.tensor_tensor(T.cm2[:], T.K2[:, 0:16].indirect(T.l1[:, 0:40]), T.QX[:], A.is_le))
+    W("t", t_c2)
+    p_2 = incs(conv(T.pD[:, 0:40], T.Wc, T.cm2, NQ, False, True))
+    W("v", p_2)
+    t_l2 = incs(v.tensor_copy(T.l2[:], T.pD[:, 0:40]))
+
+    def halves(out, win, lst, *deps):
+        W("v", *deps)
+        a = incs(v.tensor_copy(out[:, 0:320], win.indirect(lst[:, 0:20])))
+        W("s", *deps)
+        b = incs(s.activation(out[:, 320:640], win.indirect(lst[:, 20:40]), COPY))
+        return a, b
+
+    hb = halves(T.bg3, T.b3w[:, 0:256], T.l2, t_l2, s_b3)
+    W("v", t_k3)
+    t_c3 = incs(v.tensor_tensor(T.cm3[:], T.K3[:, 0:256].indirect(T.l2[:, 0:40]), T.QX[:], A.is_le))
+    W("t", c_wb, *hb)
+    conv(T.pS[:, 0:40], T.Wb, T.bg3, NQ, True, False)
+    W("t", t_c3)
+    p_3 = incs(conv(T.pS[:, 0:40], T.Wc, T.cm3, NQ, False, True))
+    W("v", p_3)
+    t_i3 = incs(v.tensor_copy(T.i3[:], T.pS[:, 0:40]))
+    hk = halves(T.kg3, T.BK[:, 0:8192], T.i3, t_i3)
+    W("t", *hk)
+    p_4 = incs(conv(T.pT[:, 0:40], T.Wk, T.kg3, NQ))
+    W("v", p_4)
+    t_m4 = incs(v.tensor_copy(T.m4[:], T.pT[:, 0:40]))
+    hb = halves(T.bg4, T.BK[:, 0:4096], T.m4, t_m4)
+    t_c4 = incs(v.tensor_tensor(T.cm4[:], T.nks[:, 0:4096].indirect(T.m4[:, 0:40]), T.QX[:], A.is_le))
+    W("t", *hb)
+    conv(T.pN[:, 0:40], T.Wb, T.bg4, NQ, True, False)
+    W("t", t_c4)
+    p_5 = incs(conv(T.pN[:, 0:40], T.Wc, T.cm4, NQ, False, True))
+    W("v", p_5)
+    t_i4 = incs(v.tensor_copy(T.i4[:], T.pN[:, 0:40]))
+    hk = halves(T.kg4, T.BK[:, 0:8192], T.i4, t_i4)
+    W("t", *hk)
+    p_6 = incs(conv(T.pA[:, 0:40], T.Wk, T.kg4, NQ))
+    W("v", p_6)
+    t_vn = incs(v.tensor_copy(T.vn[:], T.pA[:, 0:40]))
+    W("v", t_vn, d_vec)
+    W("s", t_vn, d_vec)
+
+    def vectors(call, out, r, *more):
+        return incs(call(out[:, CAP * r:CAP * r + CAP], T.vcs[:, 0:4096].indirect(T.vn[:, 10 * r:10 * r + 10]), *more))
+
+    t_an = [vectors(v.tensor_copy, T.AN, r) for r in others[:2]] + [vectors(s.activation, T.AN, others[2], COPY)]
+    s_own = vectors(s.activation, T.RX, me, COPY)
+    W("g", *t_an)
+    n_la = exchange(T.AN, T.RX, "ra", "la")
+
+    W("v", t_lb, s_own)
+    W("s", t_lb, s_own)
+    for r in others:
+        v.wait_ge(T.sem["ra%d" % r], count(r))
+        s.wait_ge(T.sem["ra%d" % r], count(r))
+    t_y = incs(v.tensor_copy(T.yb[:, 0:256], T.RX[:, 0:640].indirect(T.LB[:, 0:16])))
+    s_y = incs(s.activation(T.yb[:, 256:512], T.RX[:, 0:640].indirect(T.LB[:, 16:32]), COPY))
+    W("y", t_y)
+    d_y0 = dmas((sy, T.y[:, 0:256], T.yb[:, 0:256]))
+    W("s", s_y)
+    d_y1 = dmas((s, T.y[:, 256:512], T.yb[:, 256:512]))
+    W("y", d_y0)
+    W("s", d_y1)
+    g.wait_ge(T.sem.lq, n_lq)
+    g.wait_ge(T.sem.la, n_la)
+    W("g", *[t for t in every if t not in waited])

@@ -2,8 +2,8 @@ from concourse.bass import DstId, RemoteDMATransfer
 from concourse.mybir import dt, AluOpType, AxisListType, ActivationFunctionType
 
 CAP = 160
-NQ = 640
-NS = 128
+NS = 140
+W33 = 132
 
 SCRATCH = {
     "spi": ("sbuf", [8, 4], "int32"),
@@ -14,11 +14,11 @@ SCRATCH = {
 }
 for _dt, _bufs in (
     ("int32", "ql 32 X0 512 nks 4096 C 768 k1i 2 pid 1 pim 1 SX 640 QX 640 K2 16 K3 256"),
-    ("float32", "k1f 1 ioI 1 INC 128 U 128"),
-    ("bfloat16", "vcs 4096 BK 8192 CH 768 CL 768 ones 160 BDa 128 BD 128 NU 128 RBa 128 RB 128 CB 128 RST 128 DD 160 D0 160 D1 160 "
-                 "wt 48 Wk 144 Wb 144 Wc 144 W16 144 GE 160 MK 128 kg16 16 b2 16 kg256 256 b3w 256 cm1 640 cm2 640 cm3 640 cm4 640 "
-                 "bg3 640 bg4 640 kg3 640 kg4 640 AN 640 RX 640 yb 512"),
-    ("float16", "D0h 160 D1h 160 VAL 128 F1 64 SL 32 TT 32"),
+    ("float32", "k1f 1 ioI 1"),
+    ("bfloat16", "vcs 4096 BK 8192 CH 768 CL 768 ones 160 BDa 128 NLa 128 NL 128 NU 128 RBa 128 RB 128 CB 132 RST 132 "
+                 "DD 160 D01 320 wt 48 WW 432 ID 128 I16 128 GE 176 MK 134 kg16 16 b2 16 kg256 256 b3w 256 "
+                 "cm1 640 cm2 640 cm3 640 cm4 640 l1b 40 bg3 640 bg4 640 kg3 640 kg4 640 AN 480 RX 640 yb 512"),
+    ("float16", "D01h 320 VAL 132 F1 66 SL 32 TT 32"),
     ("uint16", "LA 32 LB 32 L16 2 LM2 2 L256 16 LM3 16 l1 40 l2 40 i3 40 m4 40 i4 40 vn 40"),
 ):
     _w = _bufs.split()
@@ -30,6 +30,9 @@ SEMAPHORES = ["s%d" % i for i in range(NS)] + ["rq%d" % i for i in range(4)] + [
 
 A = AluOpType
 COPY = ActivationFunctionType.Copy
+
+PLAN = """c1o Ta l1o c1f Tb Tc l1f c2f Td Te l2f L3f c2o i3f k3f l2o L3o m4f L4f i3o k3o i4f k4f m4o L4o vnf vef send
+ i4o k4o vno veo"""
 
 
 def rank_program(g, core, T, topo):
@@ -71,92 +74,92 @@ def rank_program(g, core, T, topo):
 
     d_ql = dmas((sy, T.ql[:], T.q[:]))
     d_sp = dmas((s, T.spi[:], T.spl[:]))
-    d_c = dmas((sy, T.C[:, 0:512], T.kid[:]), (sy, T.C[:, 512:768], T.beg[:]))
     d_k1 = dmas((s, T.k1i[:], T.nk[:, 0:2]))
     d_x0 = dmas(*[((sy, s)[o % 2], T.X0[o::16, :], T.q[:]) for o in range(16)])
-    d_na = dmas((sy, T.nks[0:64, :], T.nk[0:64, :]))
+    d_sx = dmas((sy, T.SX[:, 0:512], T.kid[:]), (s, T.SX[:, 512:640], T.beg[:, 0:2048]))
+    d_c = dmas((sy, T.C[:, 0:512], T.kid[:]), (sy, T.C[:, 512:768], T.beg[:]))
+    d_na = dmas((sy, T.nks[0:96, :], T.nk[0:96, :]))
 
     t_onef = incs(v.memset(T.onef[:], 1.0))
     t_ones = incs(v.memset(T.ones[:], 1.0))
+    t_cb0 = incs(v.memset(T.CB[:], 0.0))
+    t_rs0 = incs(v.memset(T.RST[:], 1.0))
     t_bk0 = incs(v.memset(T.BK[:, 0:2048], 0.0))
-    t_w0 = incs(*[v.memset(x[:], 0.0) for x in (T.Wk, T.Wb, T.Wc)])
-    t_ge0 = incs(v.memset(T.GE[:, 0:32], 1.0), v.memset(T.GE[:, 128:160], 0.0))
-    t_bk1 = incs(v.memset(T.BK[:, 2048:4096], 0.0))
-    t_sx = incs(v.memset(T.SX[:], 0))
+    t_mk0 = incs(v.memset(T.MK[:, 0:1], 0.0))
+
+    def fill(a, b):
+        return incs(s.activation(T.BK[:, a:b], T.BK[:, 0:b - a], COPY))
+
+    W("s", t_ones, t_cb0)
+    s_cb = incs(*[s.activation(T.CB[:, 33 * r:33 * r + 1], T.ones[:, 0:1], COPY, scale=1.25 * r) for r in (1, 2, 3)])
+    W("s", t_rs0)
+    s_rst = incs(s.activation(T.RST[:, 0:132:33], T.ones[:, 0:4], COPY, scale=0.0))
+    s_ge0 = incs(s.activation(T.GE[:, 33:166:33], T.ones[:, 0:5], COPY, scale=0.0), s.activation(T.GE[:, 1:33], T.ones[:, 0:32], COPY),
+                 s.activation(T.GE[:, 133:165], T.ones[:, 0:32], COPY, scale=0.0))
     W("s", t_bk0)
-    t_bk2 = incs(*[s.activation(T.BK[:, b:b + 2048], T.BK[:, 0:2048], COPY) for b in (4096, 6144)])
+    z = [fill(a, b) for a, b in ((2048, 4096), (4096, 6144), (6144, 7168))]
 
     def sel(out, in_, pattern, op, base, cm, *deps):
         W("g", *deps)
         return incs(g.affine_select(out, in_, pattern, op, 0.0, base, cm))
 
+    Wk, Wb, Wc = T.WW[:, 0:144], T.WW[:, 144:288], T.WW[:, 288:432]
     c = sel(T.R8a[:], T.onef[:], [[1, 128]], A.is_ge, 0, -16, t_onef)
     c_r8 = sel(T.R8[:], T.R8a[:], [[-1, 128]], A.is_ge, 15, 16, c)
     c_bda = sel(T.BDa[:], T.ones[:, 0:128], [[16, 8], [0, 16]], A.is_ge, 15, -1, t_ones)
-    c_bd = sel(T.BD[:], T.BDa[:], [[-16, 8], [0, 16]], A.is_ge, 0, 1, c_bda)
-    c_rst = sel(T.RST[:], T.ones[:, 0:128], [[0, 4], [1, 32]], A.is_gt, 0, 0, t_ones)
-    c_cb = incs(g.iota(T.CB[:], [[-10, 4], [0, 32]], 0, 0, allow_small_or_imprecise_dtypes=True))
+    c = sel(T.NLa[:], T.ones[:, 0:128], [[16, 8], [1, 16]], A.is_gt, 0, -1, t_ones)
+    c_nl = sel(T.NL[:], T.NLa[:], [[-16, 8], [0, 16]], A.is_ge, 0, 1, c)
     c_nu = sel(T.NU[:], T.BDa[:], [[-16, 8], [-1, 16]], A.is_ge, 0, 1, c_bda)
     c_dd = sel(T.DD[:], T.ones[:], [[-1, 160]], A.is_equal, 16, 1, t_ones)
-    c_d0 = sel(T.D0[:], T.DD[:], [[0, 5], [1, 32]], A.is_ge, -16, 0, c_dd)
-    c_d1 = sel(T.D1[:], T.DD[:], [[0, 5], [-1, 32]], A.is_ge, 15, 0, c_dd)
+    W("g", c_dd)
+    c_d01 = incs(g.affine_select(T.D01[:, 0:160], T.DD[:], [[0, 5], [1, 32]], A.is_ge, 0.0, -16, 0),
+                 g.affine_select(T.D01[:, 160:320], T.DD[:], [[0, 5], [-1, 32]], A.is_ge, 0.0, 15, 0))
     c_pid = incs(g.iota(T.pid[:], [[0, 1]], 0, 1))
-    wts = []
-    for k, (w, lo, hi) in enumerate(((T.Wk, 0, 1), (T.Wb, 2, 3), (T.Wc, 1, 15))):
-        c = sel(T.wt[:, 16 * k:16 * k + 9], T.ones[:, 0:9], [[-16, 9]], A.is_ge, -lo, 1, t_ones)
-        wts.append(sel(w[:, 15:144:16], T.wt[:, 16 * k:16 * k + 9], [[16, 9]], A.is_ge, hi, -1, c, t_w0))
-    c_wk, c_wb, c_wc = wts
-    c = sel(T.RBa[:], T.ones[:, 0:128], [[16, 8], [0, 16]], A.is_ge, 3, -1, t_ones)
-    c_rb = sel(T.RB[:], T.RBa[:], [[-16, 8], [0, 16]], A.is_ge, -2, 1, c)
 
     W("v", d_sp)
     t_spf = incs(v.tensor_copy(T.spf[:], T.spi[:]))
     W("t", t_spf, c_r8)
     p_sp = incs(te.matmul(T.pS[:, 0:4], T.R8[:], T.spf[:], True, True))
+    W("t", t_ones, s_cb)
+    te.matmul(T.pN[:, 0:W33], T.ones[:, 0:128], T.CB[:], True, False)
     W("v", d_ql, p_sp)
-    t_ge = incs(*[v.tensor_scalar(T.GE[:, 32 * r:32 * r + 32], T.ql[:], T.pS[:, r:r + 1], None, A.is_ge) for r in (1, 2, 3)])
-    W("v", t_ge, t_ge0)
-    t_mk = incs(v.tensor_tensor(T.MK[:], T.GE[:, 0:128], T.GE[:, 32:160], A.subtract))
-    W("t", c_bd, c_cb)
-    te.matmul(T.pN[:, 0:128], T.BD[:], T.CB[:], True, False)
-    W("t", t_mk)
-    p_t1 = incs(te.matmul(T.pT[:, 0:128], T.BD[:], T.MK[:], True, True))
-    W("t", c_nu)
-    p_n = incs(te.matmul(T.pN[:, 0:128], T.NU[:], T.MK[:], False, True))
-    W("v", d_c)
-    t_ch = incs(v.tensor_copy(T.CH[:], T.C[:]))
-    W("v", p_t1, c_rst)
-    t_inc = incs(v.tensor_tensor_scan(T.INC[:], T.RST[:], T.pT[:, 0:128], 0.0, A.mult, A.add))
-    W("v", t_inc, p_n)
-    t_u = incs(v.tensor_tensor(T.U[:], T.INC[:], T.pN[:, 0:128], A.subtract))
+    t_ge = incs(*[v.tensor_scalar(T.GE[:, 33 * r + 1:33 * r + 33], T.ql[:], T.pS[:, r:r + 1], None, A.is_ge) for r in (1, 2, 3)])
+    W("v", t_ge, s_ge0)
+    t_mk = incs(v.tensor_tensor(T.MK[:, 1:133], T.GE[:, 1:133], T.GE[:, 34:166], A.subtract))
+    W("t", t_mk, t_mk0, c_nl, c_nu)
+    te.matmul(T.pN[:, 0:W33], T.NL[:], T.MK[:, 1:133], False, False)
+    p_e = incs(te.matmul(T.pN[:, 0:W33], T.NU[:], T.MK[:, 0:132], False, True))
+    t_w0 = incs(v.memset(T.WW[:], 0.0))
+    wts = []
+    for k, (w, lo, hi) in enumerate(((Wk, 0, 1), (Wb, 2, 3), (Wc, 1, 15))):
+        c = sel(T.wt[:, 16 * k:16 * k + 9], T.ones[:, 0:9], [[-16, 9]], A.is_ge, -lo, 1, t_ones)
+        wts.append(sel(w[:, 15:144:16], T.wt[:, 16 * k:16 * k + 9], [[16, 9]], A.is_ge, hi, -1, c, t_w0))
+    c_wk, c_wb, c_wc = wts
+    c = sel(T.RBa[:], T.ones[:, 0:128], [[16, 8], [0, 16]], A.is_ge, 3, -1, t_ones)
+    c_rb = sel(T.RB[:], T.RBa[:], [[-16, 8], [0, 16]], A.is_ge, -2, 1, c)
+    W("v", p_e, s_rst)
+    t_u = incs(v.tensor_tensor_scan(T.pT[:, 0:W33], T.RST[:], T.pN[:, 0:W33], 0.0, A.mult, A.add))
     W("v", t_u, t_mk)
-    t_val = incs(v.tensor_tensor(T.VAL[:], T.MK[:], T.U[:], A.mult))
+    t_val = incs(v.tensor_tensor(T.VAL[:], T.MK[:, 1:133], T.pT[:, 0:W33], A.mult))
     W("v", t_val)
-    t_f1 = incs(v.tensor_tensor(T.F1[:], T.VAL[:, 0:64], T.VAL[:, 64:128], A.add))
+    t_f1 = incs(v.tensor_tensor(T.F1[:], T.VAL[:, 0:66], T.VAL[:, 66:132], A.add))
     W("v", t_f1)
-    t_sl = incs(v.tensor_tensor(T.SL[:], T.F1[:, 0:32], T.F1[:, 32:64], A.add))
+    t_sl = incs(v.tensor_tensor(T.SL[:], T.F1[:, 0:32], T.F1[:, 33:65], A.add))
     W("v", t_sl)
     t_tt = incs(v.transpose(T.TT[:], T.SL[:]))
-    W("v", c_d0, c_d1)
-    t_dh = incs(v.tensor_copy(T.D0h[:], T.D0[:]), v.tensor_copy(T.D1h[:], T.D1[:]))
+    W("v", c_d01)
+    t_dh = incs(v.tensor_copy(T.D01h[:], T.D01[:]))
     W("t", t_tt, t_dh)
     p_a = []
     for w in range(2):
         for gg in range(2):
-            sh = 16 + 16 * (w - gg)
-            p_a.append(te.matmul(T.pA[:, w:32:2], (T.D0h, T.D1h)[w][:, sh:sh + 128], T.TT[:, 16 * gg:16 * gg + 16], gg == 0, gg == 1))
+            sh = 160 * w + 16 + 16 * (w - gg)
+            p_a.append(te.matmul(T.pA[:, w:32:2], T.D01h[:, sh:sh + 128], T.TT[:, 16 * gg:16 * gg + 16], gg == 0, gg == 1))
     p_a = incs(*p_a[1::2])
-    W("v", t_ch)
-    t_cl = incs(v.tensor_tensor(T.CL[:], T.C[:], T.CH[:], A.subtract))
     W("v", p_a)
     t_la = incs(v.tensor_copy(T.LA[:], T.pA[:, 0:32]))
-    W("v", t_la, d_x0, t_sx)
+    W("v", t_la, d_x0, d_sx)
     t_sc = incs(v.tensor_copy(T.SX[:, 0:640].indirect(T.LA[:, 0:32]), T.X0[:]))
-
-    W("y", t_ch, t_cl, t_bk0, t_bk1, t_bk2)
-    d_bk = dmas((sy, T.BK[0::16, :], T.CH[:, 0:512]), (sy, T.BK[2::16, 0:4096], T.CH[:, 512:768]),
-                (sy, T.BK[1::16, :], T.CL[:, 0:512]), (sy, T.BK[3::16, 0:4096], T.CL[:, 512:768]))
-    d_nb = dmas((sy, T.nks[64:128, :], T.nk[64:128, :]))
 
     def engines_of(src, dst):
         away = [d for d in T.cores if topo.chip(d) != topo.chip(src)]
@@ -164,138 +167,176 @@ def rank_program(g, core, T, topo):
         if dst in away:
             n = len(ae) // len(away)
             return ae[away.index(dst) * n:away.index(dst) * n + n]
-        return [e for e in topo.engines(src, dst) if e not in ae]
+        return [e for e in topo.engines(src, dst) if e not in ae][::2]
 
     def count(r):
         return len(engines_of(T.cores[r], core))
 
-    others = sorted([r for r in range(4) if r != me], key=lambda r: topo.chip(T.cores[r]) != topo.chip(core))
+    def order(x):
+        return sorted([r for r in range(4) if r != x], key=lambda r: topo.chip(T.cores[r]) == topo.chip(T.cores[x]))
 
-    def exchange(src, dst, sem, lsem):
+    others = order(me)
+
+    def exchange(src, dst, at, to, sem, lsem):
         tr = []
         for r in others:
             d = T.cores[r]
             a = topo.addr(d)
             tr.append(RemoteDMATransfer(dst_ids=[DstId(rid=a[0], pnc=a[1])], dma_engine_mask=sum(1 << e for e in engines_of(core, d)),
-                                        remote_sem=T.sem["%s%d" % (sem, me)], src=src[:, CAP * r:CAP * r + CAP],
-                                        dst=dst[:, CAP * me:CAP * me + CAP]))
+                                        remote_sem=T.sem["%s%d" % (sem, me)], src=src[:, CAP * at(r):CAP * at(r) + CAP],
+                                        dst=dst[:, CAP * to(r):CAP * to(r) + CAP]))
         g.remote_dma_fused(tr, local_sem=T.sem[lsem])
         return sum(len(engines_of(core, T.cores[r])) for r in others)
 
     W("g", t_sc)
-    n_lq = exchange(T.SX, T.QX, "rq", "lq")
+    n_lq = exchange(T.SX, T.QX, lambda r: r, lambda r: order(r).index(me), "rq", "lq")
 
+    W("v", d_c)
+    parts = ((512, 768, T.p1), (0, 256, T.pC), (256, 512, T.pD))
+    t_ch = [incs(v.tensor_copy(T.CH[:, a:b], T.C[:, a:b])) for a, b, p in parts]
+    z.append(incs(v.memset(T.BK[:, 7168:8192], 0.0)))
+    s_h, t_cl = [], []
+    for (a, b, p), t in zip(parts, t_ch):
+        W("s", t)
+        s_h.append(incs(s.activation(p[:, 0:256], T.CH[:, a:b], COPY)))
+    for (a, b, p), t in zip(parts, s_h):
+        W("v", t)
+        t_cl.append(incs(v.tensor_tensor(T.CL[:, a:b], T.C[:, a:b], p[:, 0:256], A.subtract)))
+    W("y", *t_ch, *z, t_bk0)
+    b1 = [sy.dma_start(T.BK[2::16, 0:4096], T.CH[:, 512:768]), sy.dma_start(T.BK[0::16, :], T.CH[:, 0:512])]
+    W("y", *t_cl)
+    b1 += [sy.dma_start(T.BK[3::16, 0:4096], T.CL[:, 512:768]), sy.dma_start(T.BK[1::16, :], T.CL[:, 0:512])]
+    d_bk = incs(*b1, n=16)
+    d_nb = dmas((sy, T.nks[96:128, :], T.nk[96:128, :]))
+    d_vec = dmas((sy, T.vcs[:], T.vec[:]))
     W("v", t_sc)
-    own = slice(CAP * me, CAP * me + CAP)
-    t_ox = incs(v.tensor_copy(T.QX[:, own], T.SX[:, own]))
+    t_ox = incs(v.tensor_copy(T.QX[:, 480:640], T.SX[:, CAP * me:CAP * me + CAP]))
     W("v", d_k1)
     t_k1 = incs(v.tensor_copy(T.k1f[:], T.k1i[:, 0:1]))
     W("v", c_pid)
     t_pim = incs(v.tensor_scalar(T.pim[:], T.pid[:], 15, None, A.bitwise_and))
+    t_lb = incs(v.tensor_copy(T.LB[:], T.SL[:]))
     W("v", t_pim)
     t_io = incs(v.tensor_copy(T.ioI[:], T.pim[:]))
-    W("v", c_wc)
-    t_w16 = incs(v.tensor_scalar(T.W16[:], T.Wc[:], 16.0, None, A.mult))
-    t_lb = incs(v.tensor_copy(T.LB[:], T.SL[:]))
-    W("v", t_k1, t_ox)
-    t_c1o = incs(v.tensor_scalar(T.cm1[:, own], T.QX[:, own], T.k1f[:, 0:1], None, A.is_ge))
-    W("t", d_bk, c_rb)
-    p_b0 = incs(te.matmul(T.p1[:, 0:1], T.RB[:], T.BK[:, 0:1], True, True))
-    W("v", p_b0, t_io)
-    t_l16 = incs(v.tensor_scalar(T.L16[:, 0:1], T.p1[:, 0:1], T.ioI[:, 0:1], None, A.add))
-    W("s", t_l16, d_bk)
-    s_k16 = incs(s.activation(T.kg16[:], T.BK[:, 0:8192].indirect(T.L16[:, 0:1]), COPY))
-    W("t", s_k16, c_wk)
-    p_m2 = incs(conv(T.p2[:, 0:1], T.Wk, T.kg16, 16))
-    W("v", p_m2)
-    t_m2 = incs(v.tensor_copy(T.LM2[:, 0:1], T.p2[:, 0:1]))
-    W("s", t_m2)
-    s_b2 = incs(s.activation(T.b2[:], T.BK[:, 0:4096].indirect(T.LM2[:, 0:1]), COPY))
-    W("t", s_b2, t_l16)
-    p_b2 = incs(te.matmul(T.p1[:, 0:16], T.RB[:], T.b2[:], True, True))
-    W("v", p_b2)
-    t_l256 = incs(v.tensor_scalar(T.L256[:], T.p1[:, 0:16], T.ioI[:, 0:1], None, A.add))
-    W("s", t_l256)
-    s_k256 = incs(s.activation(T.kg256[:], T.BK[:, 0:8192].indirect(T.L256[:, 0:16]), COPY))
-    W("v", d_na, d_nb, t_m2)
-    t_k2 = incs(v.tensor_copy(T.K2[:], T.nks[:, 0:4096].indirect(T.LM2[:, 0:1])))
-    W("t", s_k256, t_m2)
-    p_m3 = incs(conv(T.p2[:, 0:16], T.Wk, T.kg256, 256))
-    W("v", p_m3)
-    t_m3 = incs(v.tensor_copy(T.LM3[:], T.p2[:, 0:16]))
-    W("s", t_m3)
-    s_b3 = incs(s.activation(T.b3w[:], T.BK[:, 0:4096].indirect(T.LM3[:, 0:16]), COPY))
-    W("v", t_m3)
-    t_k3 = incs(v.tensor_copy(T.K3[:], T.nks[:, 0:4096].indirect(T.LM3[:, 0:16])))
+    c_id = sel(T.ID[:], T.ones[:, 0:128], [[-1, 128]], A.is_equal, 0, 1, t_ones)
+    W("s", c_id)
+    s_i16 = incs(s.activation(T.I16[:], T.ID[:], COPY, scale=16.0))
 
-    t_c1 = []
-    for r in others:
-        v.wait_ge(T.sem["rq%d" % r], count(r))
-        b = slice(CAP * r, CAP * r + CAP)
-        t_c1.append(v.tensor_scalar(T.cm1[:, b], T.QX[:, b], T.k1f[:, 0:1], None, A.is_ge))
-    t_c1 = incs(*t_c1)
-    W("y", t_c1)
-    d_vec = dmas((sy, T.vcs[:], T.vec[:]))
-    W("t", c_wc, t_c1, t_c1o)
-    p_1 = incs(conv(T.pC[:, 0:40], T.Wc, T.cm1, NQ))
-    W("t", t_w16)
-    conv(T.pD[:, 0:40], T.W16, T.cm1, NQ, True, False)
-    W("v", p_1)
-    t_l1 = incs(v.tensor_copy(T.l1[:], T.pC[:, 0:40]))
-    W("v", t_l1, t_k2)
-    t_c2 = incs(v.tensor_tensor(T.cm2[:], T.K2[:, 0:16].indirect(T.l1[:, 0:40]), T.QX[:], A.is_le))
-    W("t", t_c2)
-    p_2 = incs(conv(T.pD[:, 0:40], T.Wc, T.cm2, NQ, False, True))
-    W("v", p_2)
-    t_l2 = incs(v.tensor_copy(T.l2[:], T.pD[:, 0:40]))
+    B = {"f": (0, 480, 224, (T.pD, T.pT), tuple(others)), "o": (480, 640, 480, (T.pN, T.pA), ())}
+    tok = {}
 
-    def halves(out, win, lst, *deps):
-        W("v", *deps)
-        a = incs(v.tensor_copy(out[:, 0:320], win.indirect(lst[:, 0:20])))
-        W("s", *deps)
-        b = incs(s.activation(out[:, 320:640], win.indirect(lst[:, 20:40]), COPY))
-        return a, b
+    def cols(x, b):
+        return x[:, b[0]:b[1]]
 
-    hb = halves(T.bg3, T.b3w[:, 0:256], T.l2, t_l2, s_b3)
-    W("v", t_k3)
-    t_c3 = incs(v.tensor_tensor(T.cm3[:], T.K3[:, 0:256].indirect(T.l2[:, 0:40]), T.QX[:], A.is_le))
-    W("t", c_wb, *hb)
-    conv(T.pS[:, 0:40], T.Wb, T.bg3, NQ, True, False)
-    W("t", t_c3)
-    p_3 = incs(conv(T.pS[:, 0:40], T.Wc, T.cm3, NQ, False, True))
-    W("v", p_3)
-    t_i3 = incs(v.tensor_copy(T.i3[:], T.pS[:, 0:40]))
-    hk = halves(T.kg3, T.BK[:, 0:8192], T.i3, t_i3)
-    W("t", *hk)
-    p_4 = incs(conv(T.pT[:, 0:40], T.Wk, T.kg3, NQ))
-    W("v", p_4)
-    t_m4 = incs(v.tensor_copy(T.m4[:], T.pT[:, 0:40]))
-    hb = halves(T.bg4, T.BK[:, 0:4096], T.m4, t_m4)
-    t_c4 = incs(v.tensor_tensor(T.cm4[:], T.nks[:, 0:4096].indirect(T.m4[:, 0:40]), T.QX[:], A.is_le))
-    W("t", *hb)
-    conv(T.pN[:, 0:40], T.Wb, T.bg4, NQ, True, False)
-    W("t", t_c4)
-    p_5 = incs(conv(T.pN[:, 0:40], T.Wc, T.cm4, NQ, False, True))
-    W("v", p_5)
-    t_i4 = incs(v.tensor_copy(T.i4[:], T.pN[:, 0:40]))
-    hk = halves(T.kg4, T.BK[:, 0:8192], T.i4, t_i4)
-    W("t", *hk)
-    p_6 = incs(conv(T.pA[:, 0:40], T.Wk, T.kg4, NQ))
-    W("v", p_6)
-    t_vn = incs(v.tensor_copy(T.vn[:], T.pA[:, 0:40]))
-    W("v", t_vn, d_vec)
-    W("s", t_vn, d_vec)
+    def lst(x, b):
+        return x[:, b[0] // 16:b[1] // 16]
 
-    def vectors(call, out, r, *more):
-        return incs(call(out[:, CAP * r:CAP * r + CAP], T.vcs[:, 0:4096].indirect(T.vn[:, 10 * r:10 * r + 10]), *more))
+    def bank(b, k):
+        return b[3][k % 2][:, 0:(b[1] - b[0]) // 16]
 
-    t_an = [vectors(v.tensor_copy, T.AN, r) for r in others[:2]] + [vectors(s.activation, T.AN, others[2], COPY)]
-    s_own = vectors(s.activation, T.RX, me, COPY)
-    W("g", *t_an)
-    n_la = exchange(T.AN, T.RX, "ra", "la")
+    def c1(b):
+        W("v", t_k1, t_ox)
+        for r in b[4]:
+            v.wait_ge(T.sem["rq%d" % r], count(r))
+        tok["c1", b] = incs(v.tensor_scalar(cols(T.cm1, b), cols(T.QX, b), T.k1f[:, 0:1], None, A.is_ge))
+        W("t", c_wc, *t_cl, t_la, tok["c1", b])
+        tok["p1", b] = incs(conv(bank(b, 0), Wc, cols(T.cm1, b), b[1] - b[0]))
 
-    W("v", t_lb, s_own)
-    W("s", t_lb, s_own)
+    def lists(b, pn, name, k):
+        W("v", tok[pn, b])
+        tok[name, b] = incs(v.tensor_copy(lst(T[name], b), bank(b, k)))
+
+    def c2(b):
+        W("v", tok["l1", b], tok["K2"])
+        tok["c2", b] = incs(v.tensor_tensor(cols(T.cm2, b), T.K2[:, 0:16].indirect(lst(T.l1, b)), cols(T.QX, b), A.is_le))
+        tok["lb", b] = incs(v.tensor_copy(lst(T.l1b, b), bank(b, 0)))
+        W("t", tok["c2", b])
+        conv(bank(b, 1), Wc, cols(T.cm2, b), b[1] - b[0], True, False)
+        W("t", tok["lb", b], s_i16)
+        tok["p2", b] = incs(te.matmul(bank(b, 1), T.I16[:], lst(T.l1b, b), False, True))
+
+    def level(b, lin, win, nodes, bg, cm, pn, k, *deps):
+        W("s", tok[lin, b], *deps[:1])
+        tok["b" + pn, b] = incs(s.activation(cols(bg, b), win.indirect(lst(T[lin], b)), COPY))
+        W("v", tok[lin, b], *deps[1:])
+        tok["c" + pn, b] = incs(v.tensor_tensor(cols(cm, b), nodes.indirect(lst(T[lin], b)), cols(T.QX, b), A.is_le))
+        W("t", c_wb, tok["b" + pn, b])
+        conv(bank(b, k), Wb, cols(bg, b), b[1] - b[0], True, False)
+        W("t", tok["c" + pn, b])
+        tok[pn, b] = incs(conv(bank(b, k), Wc, cols(cm, b), b[1] - b[0], False, True))
+
+    def shared(b, win, lin, out, at, *deps):
+        a = []
+        for key, lo, hi in (("s", b[2], b[1]), ("v", b[0], b[2])):
+            if lo < hi:
+                W(key, tok[lin, b], *deps)
+                x, y = out[:, lo - at:hi - at], win.indirect(T[lin][:, lo // 16:hi // 16])
+                a.append(incs(s.activation(x, y, COPY) if key == "s" else v.tensor_copy(x, y)))
+        return a
+
+    def kids(b, lin, kg, pn, k):
+        W("t", c_wk, *shared(b, T.BK[:, 0:8192], lin, kg, 0))
+        tok[pn, b] = incs(conv(bank(b, k), Wk, cols(kg, b), b[1] - b[0]))
+
+    def vectors(b):
+        own = b is B["o"]
+        tok["ve", b] = shared(b, T.vcs[:, 0:4096], "vn", T.RX[:, CAP * me:CAP * me + CAP] if own else T.AN, b[0] if own else 0, d_vec)
+
+    steps = {"c1": c1, "l1": lambda b: lists(b, "p1", "l1", 0), "c2": c2, "l2": lambda b: lists(b, "p2", "l2", 1),
+             "L3": lambda b: level(b, "l2", T.b3w[:, 0:256], T.K3[:, 0:256], T.bg3, T.cm3, "p3", 2, tok["b3"], tok["K3"]),
+             "i3": lambda b: lists(b, "p3", "i3", 2), "k3": lambda b: kids(b, "i3", T.kg3, "p4", 3),
+             "m4": lambda b: lists(b, "p4", "m4", 3),
+             "L4": lambda b: level(b, "m4", T.BK[:, 0:4096], T.nks[:, 0:4096], T.bg4, T.cm4, "p5", 4),
+             "i4": lambda b: lists(b, "p5", "i4", 4), "k4": lambda b: kids(b, "i4", T.kg4, "p6", 5),
+             "vn": lambda b: lists(b, "p6", "vn", 5), "ve": vectors}
+
+    def table(x):
+        if x == "a":
+            W("t", d_bk, c_rb, *t_cl)
+            p = incs(te.matmul(T.p1[:, 0:1], T.RB[:], T.BK[:, 0:1], True, True))
+            W("v", p, t_io)
+            tok["L16"] = incs(v.tensor_scalar(T.L16[:, 0:1], T.p1[:, 0:1], T.ioI[:, 0:1], None, A.add))
+            W("s", tok["L16"], d_bk)
+            c = incs(s.activation(T.kg16[:], T.BK[:, 0:8192].indirect(T.L16[:, 0:1]), COPY))
+            W("t", c, c_wk)
+            tok["p_m2"] = incs(conv(T.p2[:, 0:1], Wk, T.kg16, 16))
+        if x == "b":
+            W("v", tok["p_m2"])
+            tok["LM2"] = incs(v.tensor_copy(T.LM2[:, 0:1], T.p2[:, 0:1]))
+            W("s", tok["LM2"])
+            c = incs(s.activation(T.b2[:], T.BK[:, 0:4096].indirect(T.LM2[:, 0:1]), COPY))
+            W("t", c, tok["L16"])
+            tok["p_b2"] = incs(te.matmul(T.p1[:, 0:16], T.RB[:], T.b2[:], True, True))
+            W("v", d_na, d_nb, tok["LM2"])
+            tok["K2"] = incs(v.tensor_copy(T.K2[:], T.nks[:, 0:4096].indirect(T.LM2[:, 0:1])))
+        if x == "c":
+            W("v", tok["p_b2"])
+            c = incs(v.tensor_scalar(T.L256[:], T.p1[:, 0:16], T.ioI[:, 0:1], None, A.add))
+            W("s", c)
+            c = incs(s.activation(T.kg256[:], T.BK[:, 0:8192].indirect(T.L256[:, 0:16]), COPY))
+            W("t", c, tok["LM2"])
+            tok["p_m3"] = incs(conv(T.p2[:, 0:16], Wk, T.kg256, 256))
+        if x == "d":
+            W("v", tok["p_m3"])
+            tok["LM3"] = incs(v.tensor_copy(T.LM3[:], T.p2[:, 0:16]))
+            W("s", tok["LM3"])
+            tok["b3"] = incs(s.activation(T.b3w[:], T.BK[:, 0:4096].indirect(T.LM3[:, 0:16]), COPY))
+        if x == "e":
+            W("v", tok["LM3"])
+            tok["K3"] = incs(v.tensor_copy(T.K3[:], T.nks[:, 0:4096].indirect(T.LM3[:, 0:16])))
+
+    n_la = 0
+    for x in PLAN.split():
+        if x == "send":
+            W("g", *tok["ve", B["f"]])
+            n_la = exchange(T.AN, T.RX, lambda r: others.index(r), lambda r: me, "ra", "la")
+        elif x[0] == "T":
+            table(x[1])
+        else:
+            steps[x[:2]](B[x[2]])
+
+    W("v", t_lb, *tok["ve", B["o"]])
+    W("s", t_lb, *tok["ve", B["o"]])
     for r in others:
         v.wait_ge(T.sem["ra%d" % r], count(r))
         s.wait_ge(T.sem["ra%d" % r], count(r))

@@ -9,16 +9,15 @@ SCRATCH = {
     "spi": ("sbuf", [8, 4], "int32"),
     "spf": ("sbuf", [8, 4], "float32"),
     "onef": ("sbuf", [8, 128], "float32"),
-    "R8a": ("sbuf", [8, 128], "float32"),
     "R8": ("sbuf", [8, 128], "float32"),
 }
 for _dt, _bufs in (
     ("int32", "ql 32 X0 512 nks 4096 C 768 k1i 2 pid 1 pim 1 SX 640 QX 640 K2 16 K3 256"),
     ("float32", "k1f 1 ioI 1"),
-    ("bfloat16", "vcs 4096 BK 8192 CH 768 CL 768 ones 160 BDa 128 NLa 128 NL 128 NU 128 RBa 128 RB 128 CB 132 RST 132 "
-                 "DD 160 D01 320 wt 48 WW 432 ID 128 I16 128 GE 176 MK 134 kg16 16 b2 16 kg256 256 b3w 256 "
+    ("bfloat16", "vcs 4096 BK 8192 CH 768 CL 768 ones 160 BDa 128 NLa 128 NL 128 NU 128 NLm 128 NUm 128 R0 128 RBa 128 RB 128 CB 132 RST 132 "
+                 "D01 320 wt 48 WW 432 ID 128 I16 128 GE 176 MK 132 kg16 16 b2 16 kg256 256 b3w 256 "
                  "cm1 640 cm2 640 cm3 640 cm4 640 l1b 40 bg3 640 bg4 640 kg3 640 kg4 640 AN 480 RX 640 yb 512"),
-    ("float16", "D01h 320 VAL 132 F1 66 SL 32 TT 32"),
+    ("float16", "VAL 132 F1 66 SL 32 TT 32"),
     ("uint16", "LA 32 LB 32 L16 2 LM2 2 L256 16 LM3 16 l1 40 l2 40 i3 40 m4 40 i4 40 vn 40"),
 ):
     _w = _bufs.split()
@@ -85,7 +84,7 @@ def rank_program(g, core, T, topo):
     t_cb0 = incs(v.memset(T.CB[:], 0.0))
     t_rs0 = incs(v.memset(T.RST[:], 1.0))
     t_bk0 = incs(v.memset(T.BK[:, 0:2048], 0.0))
-    t_mk0 = incs(v.memset(T.MK[:, 0:1], 0.0))
+    t_mk0 = incs(v.memset(T.GE[:, 0:1], 0.0))
 
     def fill(a, b):
         return incs(s.activation(T.BK[:, a:b], T.BK[:, 0:b - a], COPY))
@@ -97,24 +96,30 @@ def rank_program(g, core, T, topo):
     s_ge0 = incs(s.activation(T.GE[:, 33:166:33], T.ones[:, 0:5], COPY, scale=0.0), s.activation(T.GE[:, 1:33], T.ones[:, 0:32], COPY),
                  s.activation(T.GE[:, 133:165], T.ones[:, 0:32], COPY, scale=0.0))
     W("s", t_bk0)
-    z = [fill(a, b) for a, b in ((2048, 4096), (4096, 6144), (6144, 7168))]
+    z = [fill(2048, 2560)]
 
     def sel(out, in_, pattern, op, base, cm, *deps):
         W("g", *deps)
         return incs(g.affine_select(out, in_, pattern, op, 0.0, base, cm))
 
     Wk, Wb, Wc = T.WW[:, 0:144], T.WW[:, 144:288], T.WW[:, 288:432]
-    c = sel(T.R8a[:], T.onef[:], [[1, 128]], A.is_ge, 0, -16, t_onef)
-    c_r8 = sel(T.R8[:], T.R8a[:], [[-1, 128]], A.is_ge, 15, 16, c)
+    c_r8 = sel(T.R8[:], T.onef[:], [[-1, 8], [0, 16]], A.is_equal, 0, 1, t_onef)
     c_bda = sel(T.BDa[:], T.ones[:, 0:128], [[16, 8], [0, 16]], A.is_ge, 15, -1, t_ones)
     c = sel(T.NLa[:], T.ones[:, 0:128], [[16, 8], [1, 16]], A.is_gt, 0, -1, t_ones)
     c_nl = sel(T.NL[:], T.NLa[:], [[-16, 8], [0, 16]], A.is_ge, 0, 1, c)
     c_nu = sel(T.NU[:], T.BDa[:], [[-16, 8], [-1, 16]], A.is_ge, 0, 1, c_bda)
-    c_dd = sel(T.DD[:], T.ones[:], [[-1, 160]], A.is_equal, 16, 1, t_ones)
-    W("g", c_dd)
-    c_d01 = incs(g.affine_select(T.D01[:, 0:160], T.DD[:], [[0, 5], [1, 32]], A.is_ge, 0.0, -16, 0),
-                 g.affine_select(T.D01[:, 160:320], T.DD[:], [[0, 5], [-1, 32]], A.is_ge, 0.0, 15, 0))
+    W("g", t_ones)
+    c_d01 = incs(g.affine_select(T.D01[:, 0:160], T.ones[:], [[-32, 5], [-1000, 2], [-1, 16]], A.is_equal, 0.0, 1000, 1),
+                 g.affine_select(T.D01[:, 160:320], T.ones[:], [[-32, 5], [-1000, 2], [-1, 16]], A.is_equal, 0.0, 16, 1))
+    W("s", c_nl)
+    s_nl = incs(s.activation(T.NLm[:], T.NL[:], COPY, scale=-1.0))
+    W("s", c_nu)
+    s_nm = incs(s.activation(T.NUm[:], T.NU[:], COPY, scale=-1.0))
+    z += [fill(a, b) for a, b in ((2560, 4608), (4608, 6656), (6656, 8192))]
     c_pid = incs(g.iota(T.pid[:], [[0, 1]], 0, 1))
+    c_r0 = sel(T.R0[:], T.ones[:, 0:128], [[-16, 8], [0, 16]], A.is_equal, 0, 1, t_ones)
+    c = sel(T.RBa[:], T.ones[:, 0:128], [[16, 8], [0, 16]], A.is_ge, 3, -1, t_ones)
+    c_rb = sel(T.RB[:], T.RBa[:], [[-16, 8], [0, 16]], A.is_ge, -2, 1, c)
 
     W("v", d_sp)
     t_spf = incs(v.tensor_copy(T.spf[:], T.spi[:]))
@@ -124,38 +129,33 @@ def rank_program(g, core, T, topo):
     te.matmul(T.pN[:, 0:W33], T.ones[:, 0:128], T.CB[:], True, False)
     W("v", d_ql, p_sp)
     t_ge = incs(*[v.tensor_scalar(T.GE[:, 33 * r + 1:33 * r + 33], T.ql[:], T.pS[:, r:r + 1], None, A.is_ge) for r in (1, 2, 3)])
+    W("t", t_ge, s_ge0, t_mk0, c_nl, c_nu)
+    te.matmul(T.pN[:, 0:W33], T.NL[:], T.GE[:, 1:133], False, False)
+    te.matmul(T.pN[:, 0:W33], T.NU[:], T.GE[:, 0:132], False, False)
+    W("t", s_nl)
+    te.matmul(T.pN[:, 0:W33], T.NLm[:], T.GE[:, 34:166], False, False)
+    W("t", s_nm)
+    p_e = incs(te.matmul(T.pN[:, 0:W33], T.NUm[:], T.GE[:, 33:165], False, True))
     W("v", t_ge, s_ge0)
-    t_mk = incs(v.tensor_tensor(T.MK[:, 1:133], T.GE[:, 1:133], T.GE[:, 34:166], A.subtract))
-    W("t", t_mk, t_mk0, c_nl, c_nu)
-    te.matmul(T.pN[:, 0:W33], T.NL[:], T.MK[:, 1:133], False, False)
-    p_e = incs(te.matmul(T.pN[:, 0:W33], T.NU[:], T.MK[:, 0:132], False, True))
-    t_w0 = incs(v.memset(T.WW[:], 0.0))
-    wts = []
-    for k, (w, lo, hi) in enumerate(((Wk, 0, 1), (Wb, 2, 3), (Wc, 1, 15))):
-        c = sel(T.wt[:, 16 * k:16 * k + 9], T.ones[:, 0:9], [[-16, 9]], A.is_ge, -lo, 1, t_ones)
-        wts.append(sel(w[:, 15:144:16], T.wt[:, 16 * k:16 * k + 9], [[16, 9]], A.is_ge, hi, -1, c, t_w0))
-    c_wk, c_wb, c_wc = wts
-    c = sel(T.RBa[:], T.ones[:, 0:128], [[16, 8], [0, 16]], A.is_ge, 3, -1, t_ones)
-    c_rb = sel(T.RB[:], T.RBa[:], [[-16, 8], [0, 16]], A.is_ge, -2, 1, c)
+    t_mk = incs(v.tensor_tensor(T.MK[:], T.GE[:, 1:133], T.GE[:, 34:166], A.subtract))
     W("v", p_e, s_rst)
     t_u = incs(v.tensor_tensor_scan(T.pT[:, 0:W33], T.RST[:], T.pN[:, 0:W33], 0.0, A.mult, A.add))
     W("v", t_u, t_mk)
-    t_val = incs(v.tensor_tensor(T.VAL[:], T.MK[:, 1:133], T.pT[:, 0:W33], A.mult))
+    t_val = incs(v.tensor_tensor(T.VAL[:], T.MK[:], T.pT[:, 0:W33], A.mult))
     W("v", t_val)
     t_f1 = incs(v.tensor_tensor(T.F1[:], T.VAL[:, 0:66], T.VAL[:, 66:132], A.add))
     W("v", t_f1)
     t_sl = incs(v.tensor_tensor(T.SL[:], T.F1[:, 0:32], T.F1[:, 33:65], A.add))
     W("v", t_sl)
     t_tt = incs(v.transpose(T.TT[:], T.SL[:]))
-    W("v", c_d01)
-    t_dh = incs(v.tensor_copy(T.D01h[:], T.D01[:]))
-    W("t", t_tt, t_dh)
+    W("t", t_tt, c_d01)
     p_a = []
     for w in range(2):
         for gg in range(2):
             sh = 160 * w + 16 + 16 * (w - gg)
-            p_a.append(te.matmul(T.pA[:, w:32:2], T.D01h[:, sh:sh + 128], T.TT[:, 16 * gg:16 * gg + 16], gg == 0, gg == 1))
+            p_a.append(te.matmul(T.pA[:, w:32:2], T.D01[:, sh:sh + 128], T.TT[:, 16 * gg:16 * gg + 16], gg == 0, gg == 1))
     p_a = incs(*p_a[1::2])
+    t_w0 = incs(v.memset(T.WW[:], 0.0))
     W("v", p_a)
     t_la = incs(v.tensor_copy(T.LA[:], T.pA[:, 0:32]))
     W("v", t_la, d_x0, d_sx)
@@ -191,17 +191,23 @@ def rank_program(g, core, T, topo):
     W("g", t_sc)
     n_lq = exchange(T.SX, T.QX, lambda r: r, lambda r: order(r).index(me), "rq", "lq")
 
+    def weights(w, n, lo, hi):
+        c = sel(T.wt[:, 16 * n:16 * n + 9], T.ones[:, 0:9], [[-16, 9]], A.is_ge, -lo, 1, t_ones)
+        return sel(w[:, 15:144:16], T.wt[:, 16 * n:16 * n + 9], [[16, 9]], A.is_ge, hi, -1, c, t_w0)
+
+    c_wc = weights(Wc, 0, 1, 15)
+    c_wk = weights(Wk, 1, 0, 1)
+    c_wb = weights(Wb, 2, 2, 3)
     W("v", d_c)
-    parts = ((512, 768, T.p1), (0, 256, T.pC), (256, 512, T.pD))
-    t_ch = [incs(v.tensor_copy(T.CH[:, a:b], T.C[:, a:b])) for a, b, p in parts]
-    z.append(incs(v.memset(T.BK[:, 7168:8192], 0.0)))
-    s_h, t_cl = [], []
-    for (a, b, p), t in zip(parts, t_ch):
-        W("s", t)
-        s_h.append(incs(s.activation(p[:, 0:256], T.CH[:, a:b], COPY)))
-    for (a, b, p), t in zip(parts, s_h):
+    parts = ((512, 768), (0, 512))
+    t_ch = [incs(v.tensor_copy(T.CH[:, a:b], T.C[:, a:b])) for a, b in parts]
+    t_cl = []
+    for (a, b), t in zip(parts, t_ch):
         W("v", t)
-        t_cl.append(incs(v.tensor_tensor(T.CL[:, a:b], T.C[:, a:b], p[:, 0:256], A.subtract)))
+        t_cl.append(incs(v.tensor_tensor(T.CL[:, a:b], T.C[:, a:b], T.CH[:, a:b], A.subtract)))
+    W("t", *t_ch[:1], *t_cl[:1], c_r0, t_la)
+    te.matmul(T.p1[:, 0:1], T.R0[:], T.CH[:, 512:513], True, False)
+    p_b0 = incs(te.matmul(T.p1[:, 0:1], T.R0[:], T.CL[:, 512:513], False, True))
     W("y", *t_ch, *z, t_bk0)
     b1 = [sy.dma_start(T.BK[2::16, 0:4096], T.CH[:, 512:768]), sy.dma_start(T.BK[0::16, :], T.CH[:, 0:512])]
     W("y", *t_cl)
@@ -218,11 +224,14 @@ def rank_program(g, core, T, topo):
     t_lb = incs(v.tensor_copy(T.LB[:], T.SL[:]))
     W("v", t_pim)
     t_io = incs(v.tensor_copy(T.ioI[:], T.pim[:]))
+    W("v", p_b0, t_io)
+    t_l16 = incs(v.tensor_scalar(T.L16[:, 0:1], T.p1[:, 0:1], T.ioI[:, 0:1], None, A.add))
     c_id = sel(T.ID[:], T.ones[:, 0:128], [[-1, 128]], A.is_equal, 0, 1, t_ones)
     W("s", c_id)
     s_i16 = incs(s.activation(T.I16[:], T.ID[:], COPY, scale=16.0))
 
-    B = {"f": (0, 480, 224, (T.pD, T.pT), tuple(others)), "o": (480, 640, 480, (T.pN, T.pA), ())}
+    B = {"f": (0, 480, 224, (T.pD, T.pT), ((320, 480, tuple(others[2:])), (0, 320, tuple(others[:2])))),
+         "o": (480, 640, 480, (T.pN, T.pA), ((480, 640, ()),))}
     tok = {}
 
     def cols(x, b):
@@ -236,10 +245,13 @@ def rank_program(g, core, T, topo):
 
     def c1(b):
         W("v", t_k1, t_ox)
-        for r in b[4]:
-            v.wait_ge(T.sem["rq%d" % r], count(r))
-        tok["c1", b] = incs(v.tensor_scalar(cols(T.cm1, b), cols(T.QX, b), T.k1f[:, 0:1], None, A.is_ge))
-        W("t", c_wc, *t_cl, t_la, tok["c1", b])
+        c = []
+        for lo, hi, those in b[4]:
+            for r in those:
+                v.wait_ge(T.sem["rq%d" % r], count(r))
+            c.append(v.tensor_scalar(T.cm1[:, lo:hi], T.QX[:, lo:hi], T.k1f[:, 0:1], None, A.is_ge))
+        tok["c1", b] = incs(*c)
+        W("t", c_wc, t_la, tok["c1", b])
         tok["p1", b] = incs(conv(bank(b, 0), Wc, cols(T.cm1, b), b[1] - b[0]))
 
     def lists(b, pn, name, k):
@@ -292,11 +304,7 @@ def rank_program(g, core, T, topo):
 
     def table(x):
         if x == "a":
-            W("t", d_bk, c_rb, *t_cl)
-            p = incs(te.matmul(T.p1[:, 0:1], T.RB[:], T.BK[:, 0:1], True, True))
-            W("v", p, t_io)
-            tok["L16"] = incs(v.tensor_scalar(T.L16[:, 0:1], T.p1[:, 0:1], T.ioI[:, 0:1], None, A.add))
-            W("s", tok["L16"], d_bk)
+            W("s", t_l16, d_bk)
             c = incs(s.activation(T.kg16[:], T.BK[:, 0:8192].indirect(T.L16[:, 0:1]), COPY))
             W("t", c, c_wk)
             tok["p_m2"] = incs(conv(T.p2[:, 0:1], Wk, T.kg16, 16))
@@ -305,7 +313,7 @@ def rank_program(g, core, T, topo):
             tok["LM2"] = incs(v.tensor_copy(T.LM2[:, 0:1], T.p2[:, 0:1]))
             W("s", tok["LM2"])
             c = incs(s.activation(T.b2[:], T.BK[:, 0:4096].indirect(T.LM2[:, 0:1]), COPY))
-            W("t", c, tok["L16"])
+            W("t", c, t_l16, c_rb)
             tok["p_b2"] = incs(te.matmul(T.p1[:, 0:16], T.RB[:], T.b2[:], True, True))
             W("v", d_na, d_nb, tok["LM2"])
             tok["K2"] = incs(v.tensor_copy(T.K2[:], T.nks[:, 0:4096].indirect(T.LM2[:, 0:1])))

from concourse.bass import DstId, RemoteDMATransfer
from concourse.mybir import dt, AluOpType, AxisListType, ActivationFunctionType

CAP = 160
NS = 140
W33 = 132

SCRATCH = {
    "spi": ("sbuf", [8, 4], "int32"),
    "spf": ("sbuf", [8, 4], "float32"),
    "onef": ("sbuf", [8, 128], "float32"),
    "R8": ("sbuf", [8, 128], "float32"),
}
for _dt, _bufs in (
    ("int32", "ql 32 X0 512 nks 4096 C 768 k1i 2 pid 1 pim 1 SX 640 QX 640 K2 16 K3 256"),
    ("float32", "k1f 1 ioI 1"),
    ("bfloat16", "vcs 4096 BK 8192 CH 768 CL 768 ones 160 BDa 128 NLa 128 NL 128 NU 128 NLm 128 NUm 128 R0 128 RBa 128 RB 128 CB 132 RST 132 "
                 "D01 320 wt 48 WW 432 ID 128 I16 128 GE 176 MK 132 kg16 16 b2 16 kg256 256 b3w 256 "
                 "cm1 640 cm2 640 cm3 640 cm4 640 l1b 40 bg3 640 bg4 640 kg3 640 kg4 640 AN 480 RX 640 yb 512"),
    ("float16", "VAL 132 F1 66 SL 32 TT 32"),
    ("uint16", "LA 32 LB 32 L16 2 LM2 2 L256 16 LM3 16 l1 40 l2 40 i3 40 m4 40 i4 40 vn 40"),
):
    _w = _bufs.split()
    for _k in range(0, len(_w), 2):
        SCRATCH[_w[_k]] = ("sbuf", [128, int(_w[_k + 1])], _dt)
for _k in "pS pT pN pA p1 p2 pC pD".split():
    SCRATCH[_k] = ("psum", [128, 512], "float32")
SEMAPHORES = ["s%d" % i for i in range(NS)] + ["rq%d" % i for i in range(4)] + ["ra%d" % i for i in range(4)] + ["lq", "la"]

A = AluOpType
COPY = ActivationFunctionType.Copy

PLAN = """c1o Ta l1o c1f Tb Tc l1f c2f Td Te l2f L3f c2o i3f k3f l2o L3o m4f L4f i3o k3o i4f k4f m4o L4o vnf vef send
 i4o k4o vno veo"""


def rank_program(g, core, T, topo):
    me = T.rank_of(core)
    if me is None:
        return
    v, s, te, sy = g.vector, g.scalar, g.tensor, g.sync
    queues = {"g": g, "v": v, "s": s, "t": te, "y": sy}
    used = [0]
    seen = {}
    waited = {}
    every = []

    def incs(*ins, n=1):
        name = "s%d" % used[0]
        used[0] += 1
        for x in ins:
            x.then_inc(T.sem[name], n)
        tok = (name, n * len(ins))
        every.append(tok)
        return tok

    def dmas(*calls):
        return incs(*[q.dma_start(out, in_) for q, out, in_ in calls], n=16)

    def W(key, *toks):
        for tok in toks:
            if (key, tok) in seen:
                continue
            seen[(key, tok)] = True
            waited[tok] = True
            queues[key].wait_ge(T.sem[tok[0]], tok[1])

    def conv(out, wt, src, n, start=True, stop=True):
        ins = None
        for i in range(16):
            ins = te.matmul(out, wt[:, 15 - i:143 - i], src[:, i:n:16], start and i == 0, stop and i == 15)
        return ins

    d_ql = dmas((sy, T.ql[:], T.q[:]))
    d_sp = dmas((s, T.spi[:], T.spl[:]))
    d_k1 = dmas((s, T.k1i[:], T.nk[:, 0:2]))
    d_x0 = dmas(*[((sy, s)[o % 2], T.X0[o::16, :], T.q[:]) for o in range(16)])
    d_sx = dmas((sy, T.SX[:, 0:512], T.kid[:]), (s, T.SX[:, 512:640], T.beg[:, 0:2048]))
    d_c = dmas((sy, T.C[:, 0:512], T.kid[:]), (sy, T.C[:, 512:768], T.beg[:]))
    d_na = dmas((sy, T.nks[0:96, :], T.nk[0:96, :]))

    t_onef = incs(v.memset(T.onef[:], 1.0))
    t_ones = incs(v.memset(T.ones[:], 1.0))
    t_cb0 = incs(v.memset(T.CB[:], 0.0))
    t_rs0 = incs(v.memset(T.RST[:], 1.0))
    t_bk0 = incs(v.memset(T.BK[:, 0:2048], 0.0))
    t_mk0 = incs(v.memset(T.GE[:, 0:1], 0.0))

    def fill(a, b):
        return incs(s.activation(T.BK[:, a:b], T.BK[:, 0:b - a], COPY))

    W("s", t_ones, t_cb0)
    s_cb = incs(*[s.activation(T.CB[:, 33 * r:33 * r + 1], T.ones[:, 0:1], COPY, scale=1.25 * r) for r in (1, 2, 3)])
    W("s", t_rs0)
    s_rst = incs(s.activation(T.RST[:, 0:132:33], T.ones[:, 0:4], COPY, scale=0.0))
    s_ge0 = incs(s.activation(T.GE[:, 33:166:33], T.ones[:, 0:5], COPY, scale=0.0), s.activation(T.GE[:, 1:33], T.ones[:, 0:32], COPY),
                 s.activation(T.GE[:, 133:165], T.ones[:, 0:32], COPY, scale=0.0))
    W("s", t_bk0)
    z = [fill(2048, 2560)]

    def sel(out, in_, pattern, op, base, cm, *deps):
        W("g", *deps)
        return incs(g.affine_select(out, in_, pattern, op, 0.0, base, cm))

    Wk, Wb, Wc = T.WW[:, 0:144], T.WW[:, 144:288], T.WW[:, 288:432]
    c_r8 = sel(T.R8[:], T.onef[:], [[-1, 8], [0, 16]], A.is_equal, 0, 1, t_onef)
    c_bda = sel(T.BDa[:], T.ones[:, 0:128], [[16, 8], [0, 16]], A.is_ge, 15, -1, t_ones)
    c = sel(T.NLa[:], T.ones[:, 0:128], [[16, 8], [1, 16]], A.is_gt, 0, -1, t_ones)
    c_nl = sel(T.NL[:], T.NLa[:], [[-16, 8], [0, 16]], A.is_ge, 0, 1, c)
    c_nu = sel(T.NU[:], T.BDa[:], [[-16, 8], [-1, 16]], A.is_ge, 0, 1, c_bda)
    W("g", t_ones)
    c_d01 = incs(g.affine_select(T.D01[:, 0:160], T.ones[:], [[-32, 5], [-1000, 2], [-1, 16]], A.is_equal, 0.0, 1000, 1),
                 g.affine_select(T.D01[:, 160:320], T.ones[:], [[-32, 5], [-1000, 2], [-1, 16]], A.is_equal, 0.0, 16, 1))
    W("s", c_nl)
    s_nl = incs(s.activation(T.NLm[:], T.NL[:], COPY, scale=-1.0))
    W("s", c_nu)
    s_nm = incs(s.activation(T.NUm[:], T.NU[:], COPY, scale=-1.0))
    z += [fill(a, b) for a, b in ((2560, 4608), (4608, 6656), (6656, 8192))]
    c_pid = incs(g.iota(T.pid[:], [[0, 1]], 0, 1))
    c_r0 = sel(T.R0[:], T.ones[:, 0:128], [[-16, 8], [0, 16]], A.is_equal, 0, 1, t_ones)
    c = sel(T.RBa[:], T.ones[:, 0:128], [[16, 8], [0, 16]], A.is_ge, 3, -1, t_ones)
    c_rb = sel(T.RB[:], T.RBa[:], [[-16, 8], [0, 16]], A.is_ge, -2, 1, c)

    W("v", d_sp)
    t_spf = incs(v.tensor_copy(T.spf[:], T.spi[:]))
    W("t", t_spf, c_r8)
    p_sp = incs(te.matmul(T.pS[:, 0:4], T.R8[:], T.spf[:], True, True))
    W("t", t_ones, s_cb)
    te.matmul(T.pN[:, 0:W33], T.ones[:, 0:128], T.CB[:], True, False)
    W("v", d_ql, p_sp)
    t_ge = incs(*[v.tensor_scalar(T.GE[:, 33 * r + 1:33 * r + 33], T.ql[:], T.pS[:, r:r + 1], None, A.is_ge) for r in (1, 2, 3)])
    W("t", t_ge, s_ge0, t_mk0, c_nl, c_nu)
    te.matmul(T.pN[:, 0:W33], T.NL[:], T.GE[:, 1:133], False, False)
    te.matmul(T.pN[:, 0:W33], T.NU[:], T.GE[:, 0:132], False, False)
    W("t", s_nl)
    te.matmul(T.pN[:, 0:W33], T.NLm[:], T.GE[:, 34:166], False, False)
    W("t", s_nm)
    p_e = incs(te.matmul(T.pN[:, 0:W33], T.NUm[:], T.GE[:, 33:165], False, True))
    W("v", t_ge, s_ge0)
    t_mk = incs(v.tensor_tensor(T.MK[:], T.GE[:, 1:133], T.GE[:, 34:166], A.subtract))
    W("v", p_e, s_rst)
    t_u = incs(v.tensor_tensor_scan(T.pT[:, 0:W33], T.RST[:], T.pN[:, 0:W33], 0.0, A.mult, A.add))
    W("v", t_u, t_mk)
    t_val = incs(v.tensor_tensor(T.VAL[:], T.MK[:], T.pT[:, 0:W33], A.mult))
    W("v", t_val)
    t_f1 = incs(v.tensor_tensor(T.F1[:], T.VAL[:, 0:66], T.VAL[:, 66:132], A.add))
    W("v", t_f1)
    t_sl = incs(v.tensor_tensor(T.SL[:], T.F1[:, 0:32], T.F1[:, 33:65], A.add))
    W("v", t_sl)
    t_tt = incs(v.transpose(T.TT[:], T.SL[:]))
    W("t", t_tt, c_d01)
    p_a = []
    for w in range(2):
        for gg in range(2):
            sh = 160 * w + 16 + 16 * (w - gg)
            p_a.append(te.matmul(T.pA[:, w:32:2], T.D01[:, sh:sh + 128], T.TT[:, 16 * gg:16 * gg + 16], gg == 0, gg == 1))
    p_a = incs(*p_a[1::2])
    t_w0 = incs(v.memset(T.WW[:], 0.0))
    W("v", p_a)
    t_la = incs(v.tensor_copy(T.LA[:], T.pA[:, 0:32]))
    W("v", t_la, d_x0, d_sx)
    t_sc = incs(v.tensor_copy(T.SX[:, 0:640].indirect(T.LA[:, 0:32]), T.X0[:]))

    def engines_of(src, dst):
        away = [d for d in T.cores if topo.chip(d) != topo.chip(src)]
        ae = topo.engines(src, away[0])
        if dst in away:
            n = len(ae) // len(away)
            return ae[away.index(dst) * n:away.index(dst) * n + n]
        return [e for e in topo.engines(src, dst) if e not in ae][::2]

    def count(r):
        return len(engines_of(T.cores[r], core))

    def order(x):
        return sorted([r for r in range(4) if r != x], key=lambda r: topo.chip(T.cores[r]) == topo.chip(T.cores[x]))

    others = order(me)

    def exchange(src, dst, at, to, sem, lsem):
        tr = []
        for r in others:
            d = T.cores[r]
            a = topo.addr(d)
            tr.append(RemoteDMATransfer(dst_ids=[DstId(rid=a[0], pnc=a[1])], dma_engine_mask=sum(1 << e for e in engines_of(core, d)),
                                        remote_sem=T.sem["%s%d" % (sem, me)], src=src[:, CAP * at(r):CAP * at(r) + CAP],
                                        dst=dst[:, CAP * to(r):CAP * to(r) + CAP]))
        g.remote_dma_fused(tr, local_sem=T.sem[lsem])
        return sum(len(engines_of(core, T.cores[r])) for r in others)

    W("g", t_sc)
    n_lq = exchange(T.SX, T.QX, lambda r: r, lambda r: order(r).index(me), "rq", "lq")

    def weights(w, n, lo, hi):
        c = sel(T.wt[:, 16 * n:16 * n + 9], T.ones[:, 0:9], [[-16, 9]], A.is_ge, -lo, 1, t_ones)
        return sel(w[:, 15:144:16], T.wt[:, 16 * n:16 * n + 9], [[16, 9]], A.is_ge, hi, -1, c, t_w0)

    c_wc = weights(Wc, 0, 1, 15)
    c_wk = weights(Wk, 1, 0, 1)
    c_wb = weights(Wb, 2, 2, 3)
    W("v", d_c)
    parts = ((512, 768), (0, 512))
    t_ch = [incs(v.tensor_copy(T.CH[:, a:b], T.C[:, a:b])) for a, b in parts]
    t_cl = []
    for (a, b), t in zip(parts, t_ch):
        W("v", t)
        t_cl.append(incs(v.tensor_tensor(T.CL[:, a:b], T.C[:, a:b], T.CH[:, a:b], A.subtract)))
    W("t", *t_ch[:1], *t_cl[:1], c_r0, t_la)
    te.matmul(T.p1[:, 0:1], T.R0[:], T.CH[:, 512:513], True, False)
    p_b0 = incs(te.matmul(T.p1[:, 0:1], T.R0[:], T.CL[:, 512:513], False, True))
    W("y", *t_ch, *z, t_bk0)
    b1 = [sy.dma_start(T.BK[2::16, 0:4096], T.CH[:, 512:768]), sy.dma_start(T.BK[0::16, :], T.CH[:, 0:512])]
    W("y", *t_cl)
    b1 += [sy.dma_start(T.BK[3::16, 0:4096], T.CL[:, 512:768]), sy.dma_start(T.BK[1::16, :], T.CL[:, 0:512])]
    d_bk = incs(*b1, n=16)
    d_nb = dmas((sy, T.nks[96:128, :], T.nk[96:128, :]))
    d_vec = dmas((sy, T.vcs[:], T.vec[:]))
    W("v", t_sc)
    t_ox = incs(v.tensor_copy(T.QX[:, 480:640], T.SX[:, CAP * me:CAP * me + CAP]))
    W("v", d_k1)
    t_k1 = incs(v.tensor_copy(T.k1f[:], T.k1i[:, 0:1]))
    W("v", c_pid)
    t_pim = incs(v.tensor_scalar(T.pim[:], T.pid[:], 15, None, A.bitwise_and))
    t_lb = incs(v.tensor_copy(T.LB[:], T.SL[:]))
    W("v", t_pim)
    t_io = incs(v.tensor_copy(T.ioI[:], T.pim[:]))
    W("v", p_b0, t_io)
    t_l16 = incs(v.tensor_scalar(T.L16[:, 0:1], T.p1[:, 0:1], T.ioI[:, 0:1], None, A.add))
    c_id = sel(T.ID[:], T.ones[:, 0:128], [[-1, 128]], A.is_equal, 0, 1, t_ones)
    W("s", c_id)
    s_i16 = incs(s.activation(T.I16[:], T.ID[:], COPY, scale=16.0))

    B = {"f": (0, 480, 224, (T.pD, T.pT), ((320, 480, tuple(others[2:])), (0, 320, tuple(others[:2])))),
         "o": (480, 640, 480, (T.pN, T.pA), ((480, 640, ()),))}
    tok = {}

    def cols(x, b):
        return x[:, b[0]:b[1]]

    def lst(x, b):
        return x[:, b[0] // 16:b[1] // 16]

    def bank(b, k):
        return b[3][k % 2][:, 0:(b[1] - b[0]) // 16]

    def c1(b):
        W("v", t_k1, t_ox)
        c = []
        for lo, hi, those in b[4]:
            for r in those:
                v.wait_ge(T.sem["rq%d" % r], count(r))
            c.append(v.tensor_scalar(T.cm1[:, lo:hi], T.QX[:, lo:hi], T.k1f[:, 0:1], None, A.is_ge))
        tok["c1", b] = incs(*c)
        W("t", c_wc, t_la, tok["c1", b])
        tok["p1", b] = incs(conv(bank(b, 0), Wc, cols(T.cm1, b), b[1] - b[0]))

    def lists(b, pn, name, k):
        W("v", tok[pn, b])
        tok[name, b] = incs(v.tensor_copy(lst(T[name], b), bank(b, k)))

    def c2(b):
        W("v", tok["l1", b], tok["K2"])
        tok["c2", b] = incs(v.tensor_tensor(cols(T.cm2, b), T.K2[:, 0:16].indirect(lst(T.l1, b)), cols(T.QX, b), A.is_le))
        tok["lb", b] = incs(v.tensor_copy(lst(T.l1b, b), bank(b, 0)))
        W("t", tok["c2", b])
        conv(bank(b, 1), Wc, cols(T.cm2, b), b[1] - b[0], True, False)
        W("t", tok["lb", b], s_i16)
        tok["p2", b] = incs(te.matmul(bank(b, 1), T.I16[:], lst(T.l1b, b), False, True))

    def level(b, lin, win, nodes, bg, cm, pn, k, *deps):
        W("s", tok[lin, b], *deps[:1])
        tok["b" + pn, b] = incs(s.activation(cols(bg, b), win.indirect(lst(T[lin], b)), COPY))
        W("v", tok[lin, b], *deps[1:])
        tok["c" + pn, b] = incs(v.tensor_tensor(cols(cm, b), nodes.indirect(lst(T[lin], b)), cols(T.QX, b), A.is_le))
        W("t", c_wb, tok["b" + pn, b])
        conv(bank(b, k), Wb, cols(bg, b), b[1] - b[0], True, False)
        W("t", tok["c" + pn, b])
        tok[pn, b] = incs(conv(bank(b, k), Wc, cols(cm, b), b[1] - b[0], False, True))

    def shared(b, win, lin, out, at, *deps):
        a = []
        for key, lo, hi in (("s", b[2], b[1]), ("v", b[0], b[2])):
            if lo < hi:
                W(key, tok[lin, b], *deps)
                x, y = out[:, lo - at:hi - at], win.indirect(T[lin][:, lo // 16:hi // 16])
                a.append(incs(s.activation(x, y, COPY) if key == "s" else v.tensor_copy(x, y)))
        return a

    def kids(b, lin, kg, pn, k):
        W("t", c_wk, *shared(b, T.BK[:, 0:8192], lin, kg, 0))
        tok[pn, b] = incs(conv(bank(b, k), Wk, cols(kg, b), b[1] - b[0]))

    def vectors(b):
        own = b is B["o"]
        tok["ve", b] = shared(b, T.vcs[:, 0:4096], "vn", T.RX[:, CAP * me:CAP * me + CAP] if own else T.AN, b[0] if own else 0, d_vec)

    steps = {"c1": c1, "l1": lambda b: lists(b, "p1", "l1", 0), "c2": c2, "l2": lambda b: lists(b, "p2", "l2", 1),
             "L3": lambda b: level(b, "l2", T.b3w[:, 0:256], T.K3[:, 0:256], T.bg3, T.cm3, "p3", 2, tok["b3"], tok["K3"]),
             "i3": lambda b: lists(b, "p3", "i3", 2), "k3": lambda b: kids(b, "i3", T.kg3, "p4", 3),
             "m4": lambda b: lists(b, "p4", "m4", 3),
             "L4": lambda b: level(b, "m4", T.BK[:, 0:4096], T.nks[:, 0:4096], T.bg4, T.cm4, "p5", 4),
             "i4": lambda b: lists(b, "p5", "i4", 4), "k4": lambda b: kids(b, "i4", T.kg4, "p6", 5),
             "vn": lambda b: lists(b, "p6", "vn", 5), "ve": vectors}

    def table(x):
        if x == "a":
            W("s", t_l16, d_bk)
            c = incs(s.activation(T.kg16[:], T.BK[:, 0:8192].indirect(T.L16[:, 0:1]), COPY))
            W("t", c, c_wk)
            tok["p_m2"] = incs(conv(T.p2[:, 0:1], Wk, T.kg16, 16))
        if x == "b":
            W("v", tok["p_m2"])
            tok["LM2"] = incs(v.tensor_copy(T.LM2[:, 0:1], T.p2[:, 0:1]))
            W("s", tok["LM2"])
            c = incs(s.activation(T.b2[:], T.BK[:, 0:4096].indirect(T.LM2[:, 0:1]), COPY))
            W("t", c, t_l16, c_rb)
            tok["p_b2"] = incs(te.matmul(T.p1[:, 0:16], T.RB[:], T.b2[:], True, True))
            W("v", d_na, d_nb, tok["LM2"])
            tok["K2"] = incs(v.tensor_copy(T.K2[:], T.nks[:, 0:4096].indirect(T.LM2[:, 0:1])))
        if x == "c":
            W("v", tok["p_b2"])
            c = incs(v.tensor_scalar(T.L256[:], T.p1[:, 0:16], T.ioI[:, 0:1], None, A.add))
            W("s", c)
            c = incs(s.activation(T.kg256[:], T.BK[:, 0:8192].indirect(T.L256[:, 0:16]), COPY))
            W("t", c, tok["LM2"])
            tok["p_m3"] = incs(conv(T.p2[:, 0:16], Wk, T.kg256, 256))
        if x == "d":
            W("v", tok["p_m3"])
            tok["LM3"] = incs(v.tensor_copy(T.LM3[:], T.p2[:, 0:16]))
            W("s", tok["LM3"])
            tok["b3"] = incs(s.activation(T.b3w[:], T.BK[:, 0:4096].indirect(T.LM3[:, 0:16]), COPY))
        if x == "e":
            W("v", tok["LM3"])
            tok["K3"] = incs(v.tensor_copy(T.K3[:], T.nks[:, 0:4096].indirect(T.LM3[:, 0:16])))

    n_la = 0
    for x in PLAN.split():
        if x == "send":
            W("g", *tok["ve", B["f"]])
            n_la = exchange(T.AN, T.RX, lambda r: others.index(r), lambda r: me, "ra", "la")
        elif x[0] == "T":
            table(x[1])
        else:
            steps[x[:2]](B[x[2]])

    W("v", t_lb, *tok["ve", B["o"]])
    W("s", t_lb, *tok["ve", B["o"]])
    for r in others:
        v.wait_ge(T.sem["ra%d" % r], count(r))
        s.wait_ge(T.sem["ra%d" % r], count(r))
    t_y = incs(v.tensor_copy(T.yb[:, 0:256], T.RX[:, 0:640].indirect(T.LB[:, 0:16])))
    s_y = incs(s.activation(T.yb[:, 256:512], T.RX[:, 0:640].indirect(T.LB[:, 16:32]), COPY))
    W("y", t_y)
    d_y0 = dmas((sy, T.y[:, 0:256], T.yb[:, 0:256]))
    W("s", s_y)
    d_y1 = dmas((s, T.y[:, 256:512], T.yb[:, 256:512]))
    W("y", d_y0)
    W("s", d_y1)
    g.wait_ge(T.sem.lq, n_lq)
    g.wait_ge(T.sem.la, n_la)
    W("g", *[t for t in every if t not in waited])
